import numpy as np, ml_dtypes
CORES = [22,46,70,150,174,198,278,302,326,406,430,454]
N = 12
import mx_ref
NC, G, S2 = 192, 2, 11
C = np.float32(0.041)
CNT = [[48,12,16,8,8,28,0,0,28,0,28,16],[36,32,36,60,8,8,4,8,0,0,0,0],[4,0,0,28,68,52,8,0,24,8,0,0],[0,36,24,0,8,4,0,4,0,16,20,80],[0,76,0,16,4,0,8,24,16,28,0,20],[16,8,12,0,24,20,36,24,0,0,52,0],[20,8,0,64,16,0,4,28,0,52,0,0],[28,0,12,0,0,52,12,0,28,32,0,28],[0,0,4,16,0,8,52,28,12,4,44,24],[0,16,44,0,0,20,44,0,36,4,16,12],[40,4,16,0,48,0,8,56,0,12,8,0],[0,0,28,0,8,0,16,20,48,36,24,12]]
OFF = [[sum(c[:e]) for e in range(N + 1)] for c in CNT]
BF = ml_dtypes.bfloat16
def cut(t, i, w=512):
    return t[:, w * i:w * i + w]
def tile(rs):
    return np.stack(rs, axis=2).reshape(128, -1).astype(BF)
def layer(w, X):
    out = []
    for i in range(G):
        for t in range(len(X)):
            p = mx_ref.matmul(mx_ref.quantize(cut(w, len(X) * i + t)), X[t])
            z = p if t == 0 else z + p
        out.append(z)
    return out
def act(Z):
    return [np.maximum(s * z, 0) * C for z in Z for s in (1, -1)]
def setup_inputs(rng):
    def f(*shape):
        return mx_ref.flush((rng.standard_normal(shape, dtype=np.float32) * np.exp2(rng.integers(-2, 3, shape[:-1] + (1,)))).astype(BF))
    gt = (0.125 + 0.875 * rng.random((N, 2, NC))).astype(BF)
    return {"gt": gt, "x": f(N, 128, 4 * NC), "w1": f(N, 128, G * 512), "w2": f(N, 128, 512)}
def setup_inputs_blocks(rng):
    d = setup_inputs(rng)
    for k in ("x", "w1", "w2"): d[k] = mx_ref.spread(d[k], rng, 4)
    return d
def setup_inputs_wide(rng):
    d = setup_inputs(rng)
    for k in ("x", "w1", "w2"): d[k] = mx_ref.flush((d[k].astype(np.float32) * np.exp2(rng.integers(-8, 9, (N, 1, 1))).astype(np.float32)).astype(BF))
    return d
def setup_inputs_zeros(rng):
    d = setup_inputs(rng); v = d["x"].reshape(N, 128, -1, 4).copy()
    v[np.broadcast_to((rng.random((N, 1, v.shape[2], 1)) < 0.33), v.shape)] = 0
    d["x"] = v.reshape(d["x"].shape)
    return d
def reference(gt, x, w1, w2):
    y = np.zeros((N, 128, NC), np.float32); g = gt.astype(np.float32)
    for e in range(N):
        f = (e - S2) % N
        t = np.concatenate([x[j][:, 4 * OFF[j][k]:4 * OFF[j][k + 1]] for k in (e, f) for j in range(N)], axis=1)
        p = mx_ref.matmul(mx_ref.quantize(w2[e]), mx_ref.quantize(tile(act(layer(w1[e], [mx_ref.quantize(t)])))))
        c = 0
        for i, k in enumerate((e, f)):
            for j in range(N):
                a, b = OFF[j][k], OFF[j][k + 1]
                y[j][:, a:b] = y[j][:, a:b] + p[:, c:c + b - a] * g[j, i, a:b]; c += b - a
    return {"y": y}

@@ -1,0 +1,388 @@
+import numpy as np
+from concourse.bass import DstId, RemoteDMATransfer
+from concourse.mybir import dt, AluOpType, ActivationFunctionType
+
+NC = 192
+C = float(np.float32(0.041))
+MINW = 128
+GAP = 48
+
+SCRATCH = {
+    "xt": ("sbuf", [128, 4 * 320], "bfloat16"),
+    "xq": ("sbuf", [128, 320], "float8_e4m3fn_x4"),
+    "xs": ("sbuf", [128, 320], "uint8"),
+    "wt": ("sbuf", [128, 1536], "bfloat16"),
+    "wq": ("sbuf", [128, 384], "float8_e4m3fn_x4"),
+    "ws": ("sbuf", [128, 384], "uint8"),
+    "fq": ("sbuf", [128, 384], "float8_e4m3fn_x4"),
+    "fs": ("sbuf", [128, 384], "uint8"),
+    "bq": ("sbuf", [128, 1024], "float8_e4m3fn_x4"),
+    "bs": ("sbuf", [128, 1024], "uint8"),
+    "out": ("sbuf", [128, 512], "float32"),
+    "ret": ("sbuf", [128, 640], "float32"),
+    "g1": ("sbuf", [1, 2 * NC], "bfloat16"),
+    "gb": ("sbuf", [128, 2 * NC], "bfloat16"),
+    "yf": ("sbuf", [128, NC], "float32"),
+    "ys": ("sbuf", [128, NC], "float32"),
+    "yb": ("sbuf", [128, NC], "float32"),
+    "z": ("psum", [128, 4 * 512], "float32"),
+    "p": ("psum", [128, 4 * 512], "float32"),
+}
+for _s in range(2):
+    for _c in range(2):
+        SCRATCH["h%d%d" % (_s, _c)] = ("sbuf", [128, 4 * 512], "bfloat16")
+        SCRATCH["hq%d%d" % (_s, _c)] = ("sbuf", [128, 512], "float8_e4m3fn_x4")
+        SCRATCH["hs%d%d" % (_s, _c)] = ("sbuf", [128, 512], "uint8")
+
+SEMAPHORES = ["xl", "wl", "gl", "xqd", "oqd", "wqd", "xa0", "xa1", "wa", "sent", "bc", "mul", "add", "yst"]
+for _s in range(2):
+    for _c in range(2):
+        SEMAPHORES += ["za%d%d" % (_s, _c), "zb%d%d" % (_s, _c), "as%d%d" % (_s, _c), "av%d%d" % (_s, _c),
+                       "hd%d%d" % (_s, _c), "pd%d%d" % (_s, _c)]
+for _i in range(6):
+    SEMAPHORES += ["cg%d" % _i, "ra%d" % _i]
+
+_cache = {}
+
+
+def bits(m):
+    return [i for i in range(16) if (m >> i) & 1]
+
+
+def share(m, n):
+    b = bits(m)
+    k = len(b) // n
+    return [sum(1 << e for e in b[k * i:k * i + k]) for i in range(n)]
+
+
+def grouping(items):
+    if len(items) <= 1:
+        return [list(items)] if items else []
+    box = [None]
+
+    def rec(rest, groups, pad, singles):
+        if not rest:
+            if box[0] is None or pad < box[0][0]:
+                box[0] = (pad, groups)
+            return
+        a = rest[0]
+        for i in range(1, len(rest)):
+            b = rest[i]
+            rec(rest[1:i] + rest[i + 1:], groups + [sorted([a, b])], pad + abs(a[0] - b[0]), singles)
+        if singles:
+            rec(rest[1:], groups + [[a]], pad, singles - 1)
+
+    rec(sorted(items), [], 0, len(items) % 2)
+    return sorted(box[0][1], key=lambda gr: (-len(gr), -gr[-1][0]))
+
+
+def make_plan(T, topo):
+    if "plan" in _cache:
+        return _cache["plan"]
+    CNT = T.tables["CNT"]
+    cores = list(T.cores)
+    N = len(cores)
+    off = [[sum(c[:e]) for e in range(N + 1)] for c in CNT]
+    rack = [topo.rack(topo.host(c)) for c in cores]
+    partner = [[q for q in range(N) if rack[q] != rack[r] and topo.chip(cores[q]) == topo.chip(cores[r])
+                and topo.may_write(cores[r], cores[q])][0] for r in range(N)]
+    base = [r if (partner[r] - r) % N == 3 else partner[r] for r in range(N)]
+    bases = sorted(set(base))
+    nruns, s0 = min((max((b - s) % N + 5 for b in bases), s) for s in range(N))
+    tl = [[sum(CNT[j][(s0 + k) % N] for k in range(i)) for i in range(nruns + 1)] for j in range(N)]
+    tlen = [t[-1] for t in tl]
+
+    def pieces(j, k):
+        i = (base[k] - s0) % N
+        two = [(tl[j][i], tl[j][i + 2]), (tl[j][i + 3], tl[j][i + 5])]
+        return two if base[k] == k else two[::-1]
+
+    peers = [[q for q in range(N) if rack[q] == rack[r] and q != r] for r in range(N)]
+    P = {"N": N, "cores": cores, "off": off, "partner": partner, "s0": s0, "nruns": nruns,
+         "tlen": tlen, "pieces": pieces, "cnt": CNT}
+
+    def hull(j, k):
+        ps = [p for p in pieces(j, k) if p[1] > p[0]]
+        return (min(p[0] for p in ps), max(p[1] for p in ps)) if ps else None
+
+    disp, src = [], {}
+    for j in range(N):
+        it = []
+        for k in peers[j]:
+            h = hull(j, k)
+            if h:
+                it.append((h[1] - h[0], k))
+        lst = []
+        for gi, gr in enumerate(grouping(it)):
+            W = gr[-1][0]
+            for _, k in gr:
+                src[j, k] = (min(hull(j, k)[0], tlen[j] - W), W, gi, len(gr))
+            lst.append((W, [k for _, k in gr]))
+        disp.append(lst)
+    P["disp"], P["src"] = disp, src
+    xpos, own, chunks = {}, [], []
+    for k in range(N):
+        snd = [j for j in peers[k] if (j, k) in src]
+        snd.sort(key=lambda j: (src[j, k][2], src[j, k][1]))
+        n0 = (len(snd) + 1) // 2
+        parts = [snd[:n0], snd[n0:]]
+        while sum(src[j, k][1] for j in parts[0]) < MINW:
+            p = min(range(len(parts[0])), key=lambda i: src[parts[0][i], k][1])
+            q = max(range(len(parts[1])), key=lambda i: src[parts[1][i], k][1])
+            parts[0][p], parts[1][q] = parts[1][q], parts[0][p]
+        h = hull(k, k)
+        w = (max(MINW, h[1] - h[0]) + 15) // 16 * 16
+        own.append((min(h[0], tlen[k] - w), w, 0))
+        xpos[k, k] = 0
+        area, x = {}, w
+        for c in (1, 0):
+            a = x if c == 0 else 0
+            for j in parts[c]:
+                xpos[j, k] = x
+                x += src[j, k][1]
+            area[c] = (a, x)
+        chunks.append((parts, area))
+    P["chunks"], P["xpos"], P["own"] = chunks, xpos, own
+    work = {}
+    for k in range(N):
+        parts, area = chunks[k]
+        for s in range(2):
+            for c in range(2):
+                ps = []
+                for j in parts[c] + ([k] if c == 1 else []):
+                    a, b = pieces(j, k)[s]
+                    if b > a:
+                        x = xpos[j, k] + a - (own[k][0] if j == k else src[j, k][0])
+                        ps.append((x, b - a, j))
+                ps.sort()
+                lo, hi = ps[0][0], ps[-1][0] + ps[-1][1]
+                if hi - lo < MINW:
+                    hi = min(area[c][1], lo + MINW)
+                    lo = min(lo, hi - MINW)
+                segs = [[x, x + w] for x, w, j in ps]
+                while len(segs) > 1:
+                    gap, i = min((segs[i + 1][0] - segs[i][1], i) for i in range(len(segs) - 1))
+                    if gap >= GAP and sum(b - a for a, b in segs) + gap > MINW:
+                        break
+                    segs[i:i + 2] = [[segs[i][0], segs[i + 1][1]]]
+                need = MINW - sum(b - a for a, b in segs)
+                for i in range(len(segs)):
+                    if need > 0:
+                        lim = segs[i + 1][0] if i + 1 < len(segs) else hi
+                        d = min(need, lim - segs[i][1])
+                        segs[i][1] += d
+                        need -= d
+                if need > 0:
+                    segs[0][0] -= need
+                hp, sg = 0, []
+                for a, b in segs:
+                    sg.append((a, b - a, hp))
+                    hp += b - a
+                loc = {}
+                for x, w, j in ps:
+                    for a, n, h in sg:
+                        if a <= x and x + w <= a + n:
+                            loc[j] = (h + x - a, w)
+                work[k, s, c] = (lo, hi - lo, sg, hp, loc)
+    P["work"] = work
+    rgroups, rinfo = [], {}
+    for k in range(N):
+        parts, _ = chunks[k]
+        lst, o = [], 0
+        for c in range(2):
+            it = [(sum(b - a for a, b in pieces(j, k)), j) for j in parts[c]]
+            for gr in grouping(it):
+                W = gr[-1][0]
+                mem = []
+                for w, j in gr:
+                    rinfo[k, j] = (o, W, len(lst), len(gr))
+                    mem.append(j)
+                    o += w
+                lst.append((c, W, mem))
+        rgroups.append(lst)
+    P["rgroups"], P["rinfo"] = rgroups, rinfo
+    rpos, rorder = {}, []
+    for j in range(N):
+        x = 0
+        hs = [k for k in peers[j] if (k, j) in rinfo]
+        hs.sort(key=lambda k: rinfo[k, j][2])
+        for k in hs:
+            rpos[k, j] = x
+            x += rinfo[k, j][1]
+        rorder.append(hs)
+    P["rpos"], P["rorder"] = rpos, rorder
+    _cache["plan"] = P
+    return P
+
+
+def rank_program(g, core, T, topo):
+    me = T.rank_of(core)
+    if me is None:
+        return
+    P = make_plan(T, topo)
+    N, cores, CNT, off = P["N"], P["cores"], P["cnt"], P["off"]
+    sem = T.sem
+    u8 = dt.uint8
+    sent = [0]
+
+    def send(pairs, remote):
+        n = len(pairs)
+        trs = []
+        for i, (d, o, a) in enumerate(pairs):
+            m = share(topo.mask(core, cores[d]), n)[i]
+            rid, pid = topo.addr(cores[d], core)
+            if n == 1:
+                g.remote_dma(o, a, remote[i], sem.sent, pid, rid, m)
+            else:
+                trs.append(RemoteDMATransfer(dst_ids=[DstId(rid=rid, pnc=pid)], dma_engine_mask=m, remote_sem=remote[i], src=a, dst=o))
+            sent[0] += len(bits(m))
+        if trs:
+            g.remote_dma_fused(trs, local_sem=sem.sent)
+
+    def engines(a, b, n):
+        return len(bits(topo.mask(cores[a], cores[b]))) // n
+
+    s0, nruns, tlen = P["s0"], P["nruns"], P["tlen"][me]
+    i, col, nload = 0, 0, 0
+    while i < nruns:
+        r = (s0 + i) % N
+        k = min(N - r, nruns - i)
+        a, b = off[me][r], off[me][r + k]
+        if b > a:
+            q = g.sync if nload % 2 == 0 else g.scalar
+            q.dma_start(T.xt[:, 4 * col:4 * (col + b - a)], T.x[:, 4 * a:4 * b]).then_inc(sem.xl, 16)
+            nload += 1
+        col += b - a
+        i += k
+    g.sync.dma_start(T.wt[:, 0:1024], T.w1[:, :]).then_inc(sem.wl, 16)
+    g.scalar.dma_start(T.wt[:, 1024:1536], T.w2[:, :]).then_inc(sem.wl, 16)
+    g.sync.dma_start(T.g1[:, :], T.gt[:, :]).then_inc(sem.gl, 16)
+
+    v = g.vector
+    v.wait_ge(sem.xl, 16 * nload)
+    v.quantize_mx(T.xq[:, 0:tlen], T.xs[:, 0:tlen], T.xt[:, 0:4 * tlen]).then_inc(sem.xqd, 1)
+    lo, w, x = P["own"][me]
+    v.quantize_mx(T.bq[:, x:x + w], T.bs[:, x:x + w], T.xt[:, 4 * lo:4 * (lo + w)]).then_inc(sem.oqd, 1)
+    v.wait_ge(sem.wl, 32)
+    v.quantize_mx(T.wq[:, :], T.ws[:, :], T.wt[:, :]).then_inc(sem.wqd, 1)
+
+    def chunk_of(j, k):
+        return 0 if j in P["chunks"][k][0][0] else 1
+
+    g.wait_ge(sem.xqd, 1)
+    for W, ds in P["disp"][me]:
+        rs = [sem["xa%d" % chunk_of(me, d)] for d in ds]
+        cod, sca = [], []
+        for d in ds:
+            a, x = P["src"][me, d][0], P["xpos"][me, d]
+            cod.append((d, T.bq[:, x:x + W].bitcast(u8), T.xq[:, a:a + W].bitcast(u8)))
+            sca.append((d, T.bs[:, x:x + W], T.xs[:, a:a + W]))
+        send(cod, rs)
+        send(sca, rs)
+    g.wait_ge(sem.wqd, 1)
+    pt = P["partner"][me]
+    send([(pt, T.fq[:, :].bitcast(u8), T.wq[:, :].bitcast(u8))], [sem.wa])
+    send([(pt, T.fs[:, :], T.ws[:, :])], [sem.wa])
+    g.wait_ge(sem.gl, 16)
+    g.partition_broadcast(T.gb[:, :], T.g1[0:1, :], 128).then_inc(sem.bc, 1)
+
+    t = g.tensor
+    parts = P["chunks"][me][0]
+    for s in range(2):
+        wq, ws = (T.wq, T.ws) if s == 0 else (T.fq, T.fs)
+        if s == 0:
+            t.wait_ge(sem.wqd, 1)
+        else:
+            t.wait_ge(sem.wa, 2 * engines(pt, me, 1))
+        for c in range(2):
+            if s == 0:
+                t.wait_ge(sem["xa%d" % c], sum(2 * engines(j, me, P["src"][j, me][3]) for j in parts[c]))
+                if c == 1:
+                    t.wait_ge(sem.oqd, 1)
+            lo, n, sg, hn, loc = P["work"][me, s, c]
+            for i in range(2):
+                bank = 512 * (2 * c + i)
+                t.matmul_mx(T.z[:, bank:bank + n], wq[:, 128 * i:128 * i + 128], ws[:, 128 * i:128 * i + 128],
+                            T.bq[:, lo:lo + n], T.bs[:, lo:lo + n], True, True).then_inc(sem["z%s%d%d" % ("ab"[i], s, c)], 1)
+        for c in range(2):
+            hn = P["work"][me, s, c][3]
+            bank = 512 * (2 * s + c)
+            t.wait_ge(sem["hd%d%d" % (s, c)], 1)
+            t.matmul_mx(T.p[:, bank:bank + hn], wq[:, 256:384], ws[:, 256:384], T["hq%d%d" % (s, c)][:, 0:hn],
+                        T["hs%d%d" % (s, c)][:, 0:hn], True, True).then_inc(sem["pd%d%d" % (s, c)], 1)
+
+    A = g.scalar
+    F = ActivationFunctionType
+    ncp = {}
+
+    def copies(s, c, f):
+        bank = 512 * (2 * s + c)
+        loc = P["work"][me, s, c][4]
+        for gi, (gc, W, mem) in enumerate(P["rgroups"][me]):
+            if gc != c:
+                continue
+            for j in mem:
+                if j in loc:
+                    h, n = loc[j]
+                    o = P["rinfo"][me, j][0]
+                    if s == 1:
+                        a, b = P["pieces"](j, me)[0]
+                        o += b - a
+                    f(T.out[:, o:o + n], T.p[:, bank + h:bank + h + n]).then_inc(sem["cg%d" % gi], 1)
+                    ncp[gi] = ncp.get(gi, 0) + 1
+
+    for s in range(2):
+        for c in range(2):
+            lo, n, sg, hn, loc = P["work"][me, s, c]
+            ht = T["h%d%d" % (s, c)]
+            A.wait_ge(sem["za%d%d" % (s, c)], 1)
+            bank = 512 * 2 * c - lo
+            for a, m, h in sg:
+                for b, sc in ((0, C), (1, -C)):
+                    A.activation(ht[:, 4 * h + b:4 * (h + m):4], T.z[:, bank + a:bank + a + m], F.Relu, scale=sc).then_inc(sem["as%d%d" % (s, c)], 1)
+            v.wait_ge(sem["zb%d%d" % (s, c)], 1)
+            bank += 512
+            for a, m, h in sg:
+                src = T.z[:, bank + a:bank + a + m]
+                v.tensor_scalar(ht[:, 4 * h + 2:4 * (h + m):4], src, 0.0, C, AluOpType.max, AluOpType.mult).then_inc(sem["av%d%d" % (s, c)], 1)
+                v.tensor_scalar(ht[:, 4 * h + 3:4 * (h + m):4], src, -C, 0.0, AluOpType.mult, AluOpType.max).then_inc(sem["av%d%d" % (s, c)], 1)
+            v.wait_ge(sem["av%d%d" % (s, c)], 2 * len(sg))
+            v.wait_ge(sem["as%d%d" % (s, c)], 2 * len(sg))
+            v.quantize_mx(T["hq%d%d" % (s, c)][:, 0:hn], T["hs%d%d" % (s, c)][:, 0:hn], ht[:, 0:4 * hn]).then_inc(sem["hd%d%d" % (s, c)], 1)
+        A.wait_ge(sem["pd%d0" % s], 1)
+        copies(s, 0, lambda o, i: A.activation(o, i, F.Copy))
+        v.wait_ge(sem["pd%d1" % s], 1)
+        copies(s, 1, lambda o, i: v.tensor_copy(o, i))
+
+    for gi, (c, W, mem) in enumerate(P["rgroups"][me]):
+        g.wait_ge(sem["cg%d" % gi], ncp[gi])
+        send([(j, T.ret[:, P["rpos"][me, j]:P["rpos"][me, j] + W], T.out[:, P["rinfo"][me, j][0]:P["rinfo"][me, j][0] + W]) for j in mem],
+             [sem["ra%d" % P["rorder"][j].index(me)] for j in mem])
+
+    nm = [0]
+
+    def gate(buf, pos, e):
+        for i, (dst, r) in enumerate(((T.yf, e), (T.ys, (e + 1) % N))):
+            n, o = CNT[me][r], off[me][r]
+            if n:
+                v.tensor_tensor(dst[:, o:o + n], buf[:, pos:pos + n], T.gb[:, NC * i + o:NC * i + o + n], AluOpType.mult).then_inc(sem.mul, 1)
+                nm[0] += 1
+                pos += n
+
+    v.wait_ge(sem.bc, 1)
+    for s in range(2):
+        loc = P["work"][me, s, 1][4]
+        if me in loc:
+            gate(T.p, 512 * (2 * s + 1) + loc[me][0], me if s == 0 else pt)
+    for idx, k in enumerate(P["rorder"][me]):
+        x = P["rpos"][k, me]
+        v.wait_ge(sem["ra%d" % idx], engines(k, me, P["rinfo"][k, me][3]))
+        a, b = P["pieces"](me, k)[0]
+        gate(T.ret, x, k)
+        gate(T.ret, x + b - a, P["partner"][k])
+    v.wait_ge(sem.mul, nm[0])
+    v.tensor_tensor(T.yb[:, :], T.yf[:, :], T.ys[:, :], AluOpType.add).then_inc(sem.add, 1)
+    g.sync.wait_ge(sem.add, 1)
+    g.sync.dma_start(T.y[:, :], T.yb[:, :]).then_inc(sem.yst, 16)
+    g.sync.wait_ge(sem.yst, 16)
+    g.wait_ge(sem.sent, sent[0])

@@ -34,7 +34,7 @@ for _s in range(2):
         SCRATCH["hq%d%d" % (_s, _c)] = ("sbuf", [128, 512], "float8_e4m3fn_x4")
         SCRATCH["hs%d%d" % (_s, _c)] = ("sbuf", [128, 512], "uint8")
 
-SEMAPHORES = ["xl", "wl", "gl", "xqd", "oqd", "wqd", "xa0", "xa1", "wa", "sent", "bc", "mul", "add", "yst"]
+SEMAPHORES = ["xl", "wl", "gl", "xqd", "oqd", "wqd", "xa0", "xa1", "wa", "wb", "sent", "bc", "mul", "add", "yst"]
 for _s in range(2):
     for _c in range(2):
         SEMAPHORES += ["za%d%d" % (_s, _c), "zb%d%d" % (_s, _c), "as%d%d" % (_s, _c), "av%d%d" % (_s, _c),
@@ -53,6 +53,10 @@ def share(m, n):
     b = bits(m)
     k = len(b) // n
     return [sum(1 << e for e in b[k * i:k * i + k]) for i in range(n)]
+
+
+def perms(q):
+    return [[q[i]] + r for i in range(len(q)) for r in perms(q[:i] + q[i + 1:])] if q else [[]]
 
 
 def grouping(items):
@@ -97,6 +101,9 @@ def make_plan(T, topo):
         two = [(tl[j][i], tl[j][i + 2]), (tl[j][i + 3], tl[j][i + 5])]
         return two if base[k] == k else two[::-1]
 
+    def both(j, k):
+        return sum(b - a for a, b in pieces(j, k))
+
     peers = [[q for q in range(N) if rack[q] == rack[r] and q != r] for r in range(N)]
     P = {"N": N, "cores": cores, "off": off, "partner": partner, "s0": s0, "nruns": nruns,
          "tlen": tlen, "pieces": pieces, "cnt": CNT}
@@ -113,23 +120,35 @@ def make_plan(T, topo):
             if h:
                 it.append((h[1] - h[0], k))
         lst = []
-        for gi, gr in enumerate(grouping(it)):
+        for gr in grouping(it):
             W = gr[-1][0]
             for _, k in gr:
-                src[j, k] = (min(hull(j, k)[0], tlen[j] - W), W, gi, len(gr))
+                src[j, k] = (min(hull(j, k)[0], tlen[j] - W), W, len(gr))
             lst.append((W, [k for _, k in gr]))
         disp.append(lst)
     P["disp"], P["src"] = disp, src
+
+    def span(js, k, mine):
+        x, ends = 0, []
+        for j in js:
+            a, b = pieces(j, k)[1]
+            if b > a:
+                ends += [x + a - src[j, k][0], x + b - src[j, k][0]]
+            x += src[j, k][1]
+        if not ends:
+            return 0
+        return ends[-1] if mine else ends[-1] - ends[0]
+
     xpos, own, chunks = {}, [], []
     for k in range(N):
         snd = [j for j in peers[k] if (j, k) in src]
-        snd.sort(key=lambda j: (src[j, k][2], src[j, k][1]))
-        n0 = (len(snd) + 1) // 2
-        parts = [snd[:n0], snd[n0:]]
-        while sum(src[j, k][1] for j in parts[0]) < MINW:
-            p = min(range(len(parts[0])), key=lambda i: src[parts[0][i], k][1])
-            q = max(range(len(parts[1])), key=lambda i: src[parts[1][i], k][1])
-            parts[0][p], parts[1][q] = parts[1][q], parts[0][p]
+
+        def worth(q):
+            w = sum(src[j, k][1] for j in q[:2])
+            return (w < MINW, max(MINW, span(q[:2], k, False)) - sum(both(j, k) for j in q[:2]), q)
+
+        q = min(perms(snd), key=worth)
+        parts = [q[:2], min(perms(q[2:]), key=lambda r: span(r, k, True))]
         h = hull(k, k)
         w = (max(MINW, h[1] - h[0]) + 15) // 16 * 16
         own.append((min(h[0], tlen[k] - w), w, 0))
@@ -185,32 +204,26 @@ def make_plan(T, topo):
                             loc[j] = (h + x - a, w)
                 work[k, s, c] = (lo, hi - lo, sg, hp, loc)
     P["work"] = work
-    rgroups, rinfo = [], {}
+    order, opos = [], {}
     for k in range(N):
-        parts, _ = chunks[k]
         lst, o = [], 0
         for c in range(2):
-            it = [(sum(b - a for a, b in pieces(j, k)), j) for j in parts[c]]
-            for gr in grouping(it):
-                W = gr[-1][0]
-                mem = []
-                for w, j in gr:
-                    rinfo[k, j] = (o, W, len(lst), len(gr))
-                    mem.append(j)
+            for w, j in sorted([(both(j, k), j) for j in chunks[k][0][c]])[::-1]:
+                if w:
+                    opos[k, j] = (o, w, len(lst))
+                    lst.append((c, j))
                     o += w
-                lst.append((c, W, mem))
-        rgroups.append(lst)
-    P["rgroups"], P["rinfo"] = rgroups, rinfo
+        order.append(lst)
     rpos, rorder = {}, []
     for j in range(N):
         x = 0
-        hs = [k for k in peers[j] if (k, j) in rinfo]
-        hs.sort(key=lambda k: rinfo[k, j][2])
+        hs = [k for k in peers[j] if (k, j) in opos]
+        hs.sort(key=lambda k: opos[k, j][2])
         for k in hs:
             rpos[k, j] = x
-            x += rinfo[k, j][1]
+            x += opos[k, j][1]
         rorder.append(hs)
-    P["rpos"], P["rorder"] = rpos, rorder
+    P["order"], P["opos"], P["rpos"], P["rorder"] = order, opos, rpos, rorder
     _cache["plan"] = P
     return P
 
@@ -239,7 +252,7 @@ def rank_program(g, core, T, topo):
         if trs:
             g.remote_dma_fused(trs, local_sem=sem.sent)
 
-    def engines(a, b, n):
+    def engines(a, b, n=1):
         return len(bits(topo.mask(cores[a], cores[b]))) // n
 
     s0, nruns, tlen = P["s0"], P["nruns"], P["tlen"][me]
@@ -266,23 +279,24 @@ def rank_program(g, core, T, topo):
     v.wait_ge(sem.wl, 32)
     v.quantize_mx(T.wq[:, :], T.ws[:, :], T.wt[:, :]).then_inc(sem.wqd, 1)
 
-    def chunk_of(j, k):
-        return 0 if j in P["chunks"][k][0][0] else 1
-
     g.wait_ge(sem.xqd, 1)
+    later = []
     for W, ds in P["disp"][me]:
-        rs = [sem["xa%d" % chunk_of(me, d)] for d in ds]
+        rs = [sem["xa%d" % (0 if me in P["chunks"][d][0][0] else 1)] for d in ds]
         cod, sca = [], []
         for d in ds:
             a, x = P["src"][me, d][0], P["xpos"][me, d]
             cod.append((d, T.bq[:, x:x + W].bitcast(u8), T.xq[:, a:a + W].bitcast(u8)))
             sca.append((d, T.bs[:, x:x + W], T.xs[:, a:a + W]))
         send(cod, rs)
+        later.append((sca, rs))
+    for sca, rs in later:
         send(sca, rs)
     g.wait_ge(sem.wqd, 1)
     pt = P["partner"][me]
-    send([(pt, T.fq[:, :].bitcast(u8), T.wq[:, :].bitcast(u8))], [sem.wa])
     send([(pt, T.fs[:, :], T.ws[:, :])], [sem.wa])
+    send([(pt, T.fq[:, 0:256].bitcast(u8), T.wq[:, 0:256].bitcast(u8))], [sem.wa])
+    send([(pt, T.fq[:, 256:384].bitcast(u8), T.wq[:, 256:384].bitcast(u8))], [sem.wb])
     g.wait_ge(sem.gl, 16)
     g.partition_broadcast(T.gb[:, :], T.g1[0:1, :], 128).then_inc(sem.bc, 1)
 
@@ -293,10 +307,10 @@ def rank_program(g, core, T, topo):
         if s == 0:
             t.wait_ge(sem.wqd, 1)
         else:
-            t.wait_ge(sem.wa, 2 * engines(pt, me, 1))
+            t.wait_ge(sem.wa, 2 * engines(pt, me))
         for c in range(2):
             if s == 0:
-                t.wait_ge(sem["xa%d" % c], sum(2 * engines(j, me, P["src"][j, me][3]) for j in parts[c]))
+                t.wait_ge(sem["xa%d" % c], sum(2 * engines(j, me, P["src"][j, me][2]) for j in parts[c]))
                 if c == 1:
                     t.wait_ge(sem.oqd, 1)
             lo, n, sg, hn, loc = P["work"][me, s, c]
@@ -304,6 +318,8 @@ def rank_program(g, core, T, topo):
                 bank = 512 * (2 * c + i)
                 t.matmul_mx(T.z[:, bank:bank + n], wq[:, 128 * i:128 * i + 128], ws[:, 128 * i:128 * i + 128],
                             T.bq[:, lo:lo + n], T.bs[:, lo:lo + n], True, True).then_inc(sem["z%s%d%d" % ("ab"[i], s, c)], 1)
+        if s == 1:
+            t.wait_ge(sem.wb, engines(pt, me))
         for c in range(2):
             hn = P["work"][me, s, c][3]
             bank = 512 * (2 * s + c)
@@ -318,18 +334,15 @@ def rank_program(g, core, T, topo):
     def copies(s, c, f):
         bank = 512 * (2 * s + c)
         loc = P["work"][me, s, c][4]
-        for gi, (gc, W, mem) in enumerate(P["rgroups"][me]):
-            if gc != c:
-                continue
-            for j in mem:
-                if j in loc:
-                    h, n = loc[j]
-                    o = P["rinfo"][me, j][0]
-                    if s == 1:
-                        a, b = P["pieces"](j, me)[0]
-                        o += b - a
-                    f(T.out[:, o:o + n], T.p[:, bank + h:bank + h + n]).then_inc(sem["cg%d" % gi], 1)
-                    ncp[gi] = ncp.get(gi, 0) + 1
+        for i, (jc, j) in enumerate(P["order"][me]):
+            if jc == c and j in loc:
+                h, n = loc[j]
+                o = P["opos"][me, j][0]
+                if s == 1:
+                    a, b = P["pieces"](j, me)[0]
+                    o += b - a
+                f(T.out[:, o:o + n], T.p[:, bank + h:bank + h + n]).then_inc(sem["cg%d" % i], 1)
+                ncp[i] = ncp.get(i, 0) + 1
 
     for s in range(2):
         for c in range(2):
@@ -354,10 +367,11 @@ def rank_program(g, core, T, topo):
         v.wait_ge(sem["pd%d1" % s], 1)
         copies(s, 1, lambda o, i: v.tensor_copy(o, i))
 
-    for gi, (c, W, mem) in enumerate(P["rgroups"][me]):
-        g.wait_ge(sem["cg%d" % gi], ncp[gi])
-        send([(j, T.ret[:, P["rpos"][me, j]:P["rpos"][me, j] + W], T.out[:, P["rinfo"][me, j][0]:P["rinfo"][me, j][0] + W]) for j in mem],
-             [sem["ra%d" % P["rorder"][j].index(me)] for j in mem])
+    for i, (c, j) in enumerate(P["order"][me]):
+        g.wait_ge(sem["cg%d" % i], ncp[i])
+        o, w, _ = P["opos"][me, j]
+        x = P["rpos"][me, j]
+        send([(j, T.ret[:, x:x + w], T.out[:, o:o + w])], [sem["ra%d" % P["rorder"][j].index(me)]])
 
     nm = [0]
 
@@ -374,9 +388,9 @@ def rank_program(g, core, T, topo):
         loc = P["work"][me, s, 1][4]
         if me in loc:
             gate(T.p, 512 * (2 * s + 1) + loc[me][0], me if s == 0 else pt)
-    for idx, k in enumerate(P["rorder"][me]):
+    for i, k in enumerate(P["rorder"][me]):
         x = P["rpos"][k, me]
-        v.wait_ge(sem["ra%d" % idx], engines(k, me, P["rinfo"][k, me][3]))
+        v.wait_ge(sem["ra%d" % i], engines(k, me))
         a, b = P["pieces"](me, k)[0]
         gate(T.ret, x, k)
         gate(T.ret, x + b - a, P["partner"][k])

@@ -6,40 +6,33 @@ NC = 192
 C = float(np.float32(0.041))
 MINW = 128
 GAP = 48
+CORES_ALL = 512
+PADMAX = 36
 
 SCRATCH = {
-    "xt": ("sbuf", [128, 4 * 320], "bfloat16"),
-    "xq": ("sbuf", [128, 320], "float8_e4m3fn_x4"),
-    "xs": ("sbuf", [128, 320], "uint8"),
+    "xt": ("sbuf", [128, 4 * 288], "bfloat16"),
     "wt": ("sbuf", [128, 1536], "bfloat16"),
     "wq": ("sbuf", [128, 384], "float8_e4m3fn_x4"),
     "ws": ("sbuf", [128, 384], "uint8"),
-    "fq": ("sbuf", [128, 384], "float8_e4m3fn_x4"),
-    "fs": ("sbuf", [128, 384], "uint8"),
     "bq": ("sbuf", [128, 1024], "float8_e4m3fn_x4"),
     "bs": ("sbuf", [128, 1024], "uint8"),
+    "h": ("sbuf", [128, 4 * 512], "bfloat16"),
+    "hq": ("sbuf", [128, 512], "float8_e4m3fn_x4"),
+    "hs": ("sbuf", [128, 512], "uint8"),
     "out": ("sbuf", [128, 512], "float32"),
-    "ret": ("sbuf", [128, 640], "float32"),
+    "ret": ("sbuf", [128, 768], "float32"),
     "g1": ("sbuf", [1, 2 * NC], "bfloat16"),
     "gb": ("sbuf", [128, 2 * NC], "bfloat16"),
     "yf": ("sbuf", [128, NC], "float32"),
     "ys": ("sbuf", [128, NC], "float32"),
     "yb": ("sbuf", [128, NC], "float32"),
-    "z": ("psum", [128, 4 * 512], "float32"),
-    "p": ("psum", [128, 4 * 512], "float32"),
+    "z": ("psum", [128, 2 * 512], "float32"),
+    "p": ("psum", [128, 2 * 512], "float32"),
 }
-for _s in range(2):
-    for _c in range(2):
-        SCRATCH["h%d%d" % (_s, _c)] = ("sbuf", [128, 4 * 512], "bfloat16")
-        SCRATCH["hq%d%d" % (_s, _c)] = ("sbuf", [128, 512], "float8_e4m3fn_x4")
-        SCRATCH["hs%d%d" % (_s, _c)] = ("sbuf", [128, 512], "uint8")
 
-SEMAPHORES = ["xl", "wl", "gl", "xqd", "oqd", "wqd", "xa0", "xa1", "wa", "wb", "sent", "bc", "mul", "add", "yst"]
-for _s in range(2):
-    for _c in range(2):
-        SEMAPHORES += ["za%d%d" % (_s, _c), "zb%d%d" % (_s, _c), "as%d%d" % (_s, _c), "av%d%d" % (_s, _c),
-                       "hd%d%d" % (_s, _c), "pd%d%d" % (_s, _c)]
-for _i in range(6):
+SEMAPHORES = ["xl", "wl", "wm", "gl", "xqd", "wqd", "xh", "xhs", "xa", "wa", "wb", "za", "zb", "as", "av", "hd",
+              "pd0", "pd1", "sent", "bc", "mul", "add", "yst"]
+for _i in range(12):
     SEMAPHORES += ["cg%d" % _i, "ra%d" % _i]
 
 _cache = {}
@@ -59,25 +52,20 @@ def perms(q):
     return [[q[i]] + r for i in range(len(q)) for r in perms(q[:i] + q[i + 1:])] if q else [[]]
 
 
-def grouping(items):
-    if len(items) <= 1:
-        return [list(items)] if items else []
-    box = [None]
+def splits(items, sizes):
+    if not items:
+        return [[]]
+    res, a, rest = [], items[0], items[1:]
 
-    def rec(rest, groups, pad, singles):
-        if not rest:
-            if box[0] is None or pad < box[0][0]:
-                box[0] = (pad, groups)
-            return
-        a = rest[0]
-        for i in range(1, len(rest)):
-            b = rest[i]
-            rec(rest[1:i] + rest[i + 1:], groups + [sorted([a, b])], pad + abs(a[0] - b[0]), singles)
-        if singles:
-            rec(rest[1:], groups + [[a]], pad, singles - 1)
+    def choose(q, n):
+        if n == 0:
+            return [[]]
+        return [[q[i]] + r for i in range(len(q)) for r in choose(q[i + 1:], n - 1)]
 
-    rec(sorted(items), [], 0, len(items) % 2)
-    return sorted(box[0][1], key=lambda gr: (-len(gr), -gr[-1][0]))
+    for n in sizes:
+        for c in choose(rest, n - 1):
+            res += [[[a] + c] + r for r in splits([x for x in rest if x not in c], sizes)]
+    return res
 
 
 def make_plan(T, topo):
@@ -90,160 +78,159 @@ def make_plan(T, topo):
     rack = [topo.rack(topo.host(c)) for c in cores]
     partner = [[q for q in range(N) if rack[q] != rack[r] and topo.chip(cores[q]) == topo.chip(cores[r])
                 and topo.may_write(cores[r], cores[q])][0] for r in range(N)]
-    base = [r if (partner[r] - r) % N == 3 else partner[r] for r in range(N)]
-    bases = sorted(set(base))
-    nruns, s0 = min((max((b - s) % N + 5 for b in bases), s) for s in range(N))
-    tl = [[sum(CNT[j][(s0 + k) % N] for k in range(i)) for i in range(nruns + 1)] for j in range(N)]
-    tlen = [t[-1] for t in tl]
-
-    def pieces(j, k):
-        i = (base[k] - s0) % N
-        two = [(tl[j][i], tl[j][i + 2]), (tl[j][i + 3], tl[j][i + 5])]
-        return two if base[k] == k else two[::-1]
-
-    def both(j, k):
-        return sum(b - a for a, b in pieces(j, k))
-
     peers = [[q for q in range(N) if rack[q] == rack[r] and q != r] for r in range(N)]
-    P = {"N": N, "cores": cores, "off": off, "partner": partner, "s0": s0, "nruns": nruns,
-         "tlen": tlen, "pieces": pieces, "cnt": CNT}
+    hcore, rcore = [], []
+    for r in range(N):
+        ok = [c for c in range(CORES_ALL) if topo.host(c) == topo.host(cores[r]) and topo.chip(c) == topo.chip(cores[r])
+              and c != cores[r] and all(topo.may_write(c, cores[q]) for q in peers[r])]
+        hcore.append([c for c in ok if topo.die(c) != topo.die(cores[r])][0])
+        rcore.append([c for c in ok if topo.die(c) == topo.die(cores[r])][0])
+    unit = {}
+    for r in range(N):
+        unit[r, 0], unit[r, 1] = cores[r], hcore[r]
+    expert = {(r, s): (r, partner[r])[s] for r in range(N) for s in range(2)}
+    half = N // 2
+    s0 = [min(partner[q] for q in range(N) if rack[q] == rack[j]) for j in range(N)]
+    tl = [[sum(CNT[j][(s0[j] + k) % N] for k in range(i)) for i in range(N + 2)] for j in range(N)]
+    tlen = [(tl[j][N + 1] + 15) // 16 * 16 for j in range(N)]
+    hw = [max(MINW, tl[j][half + 1], tl[j][N + 1] - tl[j][half]) for j in range(N)]
 
-    def hull(j, k):
-        ps = [p for p in pieces(j, k) if p[1] > p[0]]
-        return (min(p[0] for p in ps), max(p[1] for p in ps)) if ps else None
+    def win(j, u):
+        i = (expert[u] - s0[j]) % N
+        return tl[j][i], tl[j][i + 2]
 
-    disp, src = [], {}
+    def width(j, u):
+        a, b = win(j, u)
+        return b - a
+
+    CALL, ROW, BYTE = 300.0, 20.0, 1 / 15.0
+
+    disp, src = {}, {}
     for j in range(N):
-        it = []
-        for k in peers[j]:
-            h = hull(j, k)
-            if h:
-                it.append((h[1] - h[0], k))
-        lst = []
-        for gr in grouping(it):
-            W = gr[-1][0]
-            for _, k in gr:
-                src[j, k] = (min(hull(j, k)[0], tlen[j] - W), W, len(gr))
-            lst.append((W, [k for _, k in gr]))
-        disp.append(lst)
-    P["disp"], P["src"] = disp, src
-
-    def span(js, k, mine):
-        x, ends = 0, []
-        for j in js:
-            a, b = pieces(j, k)[1]
-            if b > a:
-                ends += [x + a - src[j, k][0], x + b - src[j, k][0]]
-            x += src[j, k][1]
-        if not ends:
-            return 0
-        return ends[-1] if mine else ends[-1] - ends[0]
-
-    xpos, own, chunks = {}, [], []
-    for k in range(N):
-        snd = [j for j in peers[k] if (j, k) in src]
-
-        def worth(q):
-            w = sum(src[j, k][1] for j in q[:2])
-            return (w < MINW, max(MINW, span(q[:2], k, False)) - sum(both(j, k) for j in q[:2]), q)
-
-        q = min(perms(snd), key=worth)
-        parts = [q[:2], min(perms(q[2:]), key=lambda r: span(r, k, True))]
-        h = hull(k, k)
-        w = (max(MINW, h[1] - h[0]) + 15) // 16 * 16
-        own.append((min(h[0], tlen[k] - w), w, 0))
-        xpos[k, k] = 0
-        area, x = {}, w
-        for c in (1, 0):
-            a = x if c == 0 else 0
-            for j in parts[c]:
-                xpos[j, k] = x
-                x += src[j, k][1]
-            area[c] = (a, x)
-        chunks.append((parts, area))
-    P["chunks"], P["xpos"], P["own"] = chunks, xpos, own
-    work = {}
-    for k in range(N):
-        parts, area = chunks[k]
         for s in range(2):
-            for c in range(2):
-                ps = []
-                for j in parts[c] + ([k] if c == 1 else []):
-                    a, b = pieces(j, k)[s]
-                    if b > a:
-                        x = xpos[j, k] + a - (own[k][0] if j == k else src[j, k][0])
-                        ps.append((x, b - a, j))
-                ps.sort()
+            items = [(width(j, (k, s)), k) for k in peers[j] if width(j, (k, s))]
+
+            def cost(gs):
+                return sum(2 * CALL + 16 * len(q) * (2 * ROW + 5 * BYTE * max(q)[0]) for q in gs)
+
+            gs = min(splits(items, (1, 2, 4)), key=cost)
+            gs.sort(key=lambda q: (-len(q), -max(q)[0]))
+            end = hw[j] if s == 1 else tl[j][N + 1]
+            lst = []
+            for q in gs:
+                W = max(q)[0]
+                for _, k in q:
+                    src[j, (k, s)] = (min(win(j, (k, s))[0], end - W), W, len(q))
+                lst.append((W, [k for _, k in q]))
+            disp[j, s] = lst
+
+    xpos, work = {}, {}
+    for k in range(N):
+        for s in range(2):
+            u = (k, s)
+            base = tlen[k] if s == 0 else hw[k]
+            best = None
+            for q in perms([j for j in peers[k] if (j, u) in src]):
+                x, pos, ps = base, {}, []
+                if width(k, u):
+                    ps.append((win(k, u)[0], width(k, u), k))
+                for j in q:
+                    pos[j] = x
+                    ps.append((x + win(j, u)[0] - src[j, u][0], width(j, u), j))
+                    x += src[j, u][1]
                 lo, hi = ps[0][0], ps[-1][0] + ps[-1][1]
-                if hi - lo < MINW:
-                    hi = min(area[c][1], lo + MINW)
-                    lo = min(lo, hi - MINW)
-                segs = [[x, x + w] for x, w, j in ps]
+                segs = [[a, a + w] for a, w, _ in ps]
                 while len(segs) > 1:
                     gap, i = min((segs[i + 1][0] - segs[i][1], i) for i in range(len(segs) - 1))
                     if gap >= GAP and sum(b - a for a, b in segs) + gap > MINW:
                         break
                     segs[i:i + 2] = [[segs[i][0], segs[i + 1][1]]]
                 need = MINW - sum(b - a for a, b in segs)
-                for i in range(len(segs)):
+                for i in range(len(segs) - 1):
                     if need > 0:
-                        lim = segs[i + 1][0] if i + 1 < len(segs) else hi
-                        d = min(need, lim - segs[i][1])
+                        d = min(need, segs[i + 1][0] - segs[i][1])
                         segs[i][1] += d
                         need -= d
                 if need > 0:
                     segs[0][0] -= need
-                hp, sg = 0, []
+                lo = min(lo, segs[0][0], hi - MINW)
+                hn, sg = 0, []
                 for a, b in segs:
-                    sg.append((a, b - a, hp))
-                    hp += b - a
-                loc = {}
-                for x, w, j in ps:
-                    for a, n, h in sg:
-                        if a <= x and x + w <= a + n:
-                            loc[j] = (h + x - a, w)
-                work[k, s, c] = (lo, hi - lo, sg, hp, loc)
-    P["work"] = work
-    order, opos = [], {}
+                    sg.append((a, b - a, hn))
+                    hn += b - a
+                c = 1.7 * (hi - lo) + 2.6 * hn + 110 * len(sg)
+                if best is None or c < best[0]:
+                    loc = {}
+                    for x1, w, j in ps:
+                        for a, n, h in sg:
+                            if a <= x1 and x1 + w <= a + n:
+                                loc[j] = (h + x1 - a, w)
+                    best = (c, pos, (lo, hi - lo, sg, hn, loc))
+            xpos[u], w = best[1], best[2]
+            hn, loc = w[3], w[4]
+            cut = min([h for h, _ in loc.values()] + [hn], key=lambda b: abs(2 * b - hn))
+            work[u] = w + (cut, max(cut, MINW), min(cut, hn - MINW))
+    order, opos = {}, {}
     for k in range(N):
-        lst, o = [], 0
-        for c in range(2):
-            for w, j in sorted([(both(j, k), j) for j in chunks[k][0][c]])[::-1]:
-                if w:
-                    opos[k, j] = (o, w, len(lst))
-                    lst.append((c, j))
+        for s in range(2):
+            u = (k, s)
+            items = [(width(j, u), j) for j in peers[k] if width(j, u)]
+            cand = []
+            for gs in splits(items, (1, 2)):
+                pad = sum(max(q)[0] - w for q in gs for w, _ in q)
+                if pad <= PADMAX:
+                    cand.append((sum(CALL + 16 * len(q) * (ROW + 4 * BYTE * max(q)[0]) for q in gs), gs))
+            gs = min(cand, key=lambda c: c[0])[1]
+            gs.sort(key=lambda q: -max(q)[0])
+            if s == 1 and width(k, u):
+                gs.append([(width(k, u), k)])
+            o, lst = 0, []
+            for i, q in enumerate(gs):
+                q.sort()
+                W = max(q)[0]
+                for w, j in q:
+                    opos[u, j] = (o, w, W, i, len(q))
                     o += w
-        order.append(lst)
+                lst.append((W, [j for _, j in q]))
+            order[u] = lst
     rpos, rorder = {}, []
     for j in range(N):
+        us = [(k, s) for k in range(N) for s in range(2) if ((k, s), j) in opos]
+        us.sort(key=lambda u: (opos[u, j][3], u[1], u[0]))
         x = 0
-        hs = [k for k in peers[j] if (k, j) in opos]
-        hs.sort(key=lambda k: opos[k, j][2])
-        for k in hs:
-            rpos[k, j] = x
-            x += opos[k, j][1]
-        rorder.append(hs)
-    P["order"], P["opos"], P["rpos"], P["rorder"] = order, opos, rpos, rorder
+        for u in us:
+            rpos[u, j] = x
+            x += opos[u, j][2]
+        rorder.append(us)
+    role = {}
+    for r in range(N):
+        role[cores[r]], role[hcore[r]], role[rcore[r]] = (r, "A"), (r, "H"), (r, "R")
+    P = {"N": N, "cores": cores, "off": off, "partner": partner, "hcore": hcore, "rcore": rcore, "unit": unit,
+         "expert": expert, "s0": s0, "tl": tl, "tlen": tlen, "hw": hw, "disp": disp, "src": src, "xpos": xpos, "work": work,
+         "order": order, "opos": opos, "rpos": rpos, "rorder": rorder, "cnt": CNT, "role": role}
     _cache["plan"] = P
     return P
 
 
 def rank_program(g, core, T, topo):
-    me = T.rank_of(core)
-    if me is None:
-        return
     P = make_plan(T, topo)
+    if core not in P["role"]:
+        return
+    me, role = P["role"][core]
     N, cores, CNT, off = P["N"], P["cores"], P["cnt"], P["off"]
+    unit, expert, hcore, rcore = P["unit"], P["expert"], P["hcore"], P["rcore"]
     sem = T.sem
     u8 = dt.uint8
     sent = [0]
+    slot = 1 if role == "H" else 0
+    u = (me, slot)
 
-    def send(pairs, remote):
+    def send(pairs, remote, masks=None):
         n = len(pairs)
         trs = []
         for i, (d, o, a) in enumerate(pairs):
-            m = share(topo.mask(core, cores[d]), n)[i]
-            rid, pid = topo.addr(cores[d], core)
+            m = masks[i] if masks else share(topo.mask(core, d), n)[i]
+            rid, pid = topo.addr(d, core)
             if n == 1:
                 g.remote_dma(o, a, remote[i], sem.sent, pid, rid, m)
             else:
@@ -253,150 +240,134 @@ def rank_program(g, core, T, topo):
             g.remote_dma_fused(trs, local_sem=sem.sent)
 
     def engines(a, b, n=1):
-        return len(bits(topo.mask(cores[a], cores[b]))) // n
+        return len(bits(topo.mask(a, b))) // n
 
-    s0, nruns, tlen = P["s0"], P["nruns"], P["tlen"][me]
-    i, col, nload = 0, 0, 0
-    while i < nruns:
-        r = (s0 + i) % N
-        k = min(N - r, nruns - i)
-        a, b = off[me][r], off[me][r + k]
-        if b > a:
-            q = g.sync if nload % 2 == 0 else g.scalar
-            q.dma_start(T.xt[:, 4 * col:4 * (col + b - a)], T.x[:, 4 * a:4 * b]).then_inc(sem.xl, 16)
-            nload += 1
-        col += b - a
-        i += k
-    g.sync.dma_start(T.wt[:, 0:1024], T.w1[:, :]).then_inc(sem.wl, 16)
-    g.scalar.dma_start(T.wt[:, 1024:1536], T.w2[:, :]).then_inc(sem.wl, 16)
-    g.sync.dma_start(T.g1[:, :], T.gt[:, :]).then_inc(sem.gl, 16)
+    def codes(x, w):
+        return T.bq[:, x:x + w].bitcast(u8)
 
-    v = g.vector
-    v.wait_ge(sem.xl, 16 * nload)
-    v.quantize_mx(T.xq[:, 0:tlen], T.xs[:, 0:tlen], T.xt[:, 0:4 * tlen]).then_inc(sem.xqd, 1)
-    lo, w, x = P["own"][me]
-    v.quantize_mx(T.bq[:, x:x + w], T.bs[:, x:x + w], T.xt[:, 4 * lo:4 * (lo + w)]).then_inc(sem.oqd, 1)
-    v.wait_ge(sem.wl, 32)
-    v.quantize_mx(T.wq[:, :], T.ws[:, :], T.wt[:, :]).then_inc(sem.wqd, 1)
+    def scales(x, w):
+        return T.bs[:, x:x + w]
 
-    g.wait_ge(sem.xqd, 1)
-    later = []
-    for W, ds in P["disp"][me]:
-        rs = [sem["xa%d" % (0 if me in P["chunks"][d][0][0] else 1)] for d in ds]
-        cod, sca = [], []
-        for d in ds:
-            a, x = P["src"][me, d][0], P["xpos"][me, d]
-            cod.append((d, T.bq[:, x:x + W].bitcast(u8), T.xq[:, a:a + W].bitcast(u8)))
-            sca.append((d, T.bs[:, x:x + W], T.xs[:, a:a + W]))
-        send(cod, rs)
-        later.append((sca, rs))
-    for sca, rs in later:
-        send(sca, rs)
-    g.wait_ge(sem.wqd, 1)
-    pt = P["partner"][me]
-    send([(pt, T.fs[:, :], T.ws[:, :])], [sem.wa])
-    send([(pt, T.fq[:, 0:256].bitcast(u8), T.wq[:, 0:256].bitcast(u8))], [sem.wa])
-    send([(pt, T.fq[:, 256:384].bitcast(u8), T.wq[:, 256:384].bitcast(u8))], [sem.wb])
-    g.wait_ge(sem.gl, 16)
-    g.partition_broadcast(T.gb[:, :], T.g1[0:1, :], 128).then_inc(sem.bc, 1)
-
-    t = g.tensor
-    parts = P["chunks"][me][0]
-    for s in range(2):
-        wq, ws = (T.wq, T.ws) if s == 0 else (T.fq, T.fs)
-        if s == 0:
-            t.wait_ge(sem.wqd, 1)
-        else:
-            t.wait_ge(sem.wa, 2 * engines(pt, me))
-        for c in range(2):
-            if s == 0:
-                t.wait_ge(sem["xa%d" % c], sum(2 * engines(j, me, P["src"][j, me][2]) for j in parts[c]))
-                if c == 1:
-                    t.wait_ge(sem.oqd, 1)
-            lo, n, sg, hn, loc = P["work"][me, s, c]
-            for i in range(2):
-                bank = 512 * (2 * c + i)
-                t.matmul_mx(T.z[:, bank:bank + n], wq[:, 128 * i:128 * i + 128], ws[:, 128 * i:128 * i + 128],
-                            T.bq[:, lo:lo + n], T.bs[:, lo:lo + n], True, True).then_inc(sem["z%s%d%d" % ("ab"[i], s, c)], 1)
-        if s == 1:
-            t.wait_ge(sem.wb, engines(pt, me))
-        for c in range(2):
-            hn = P["work"][me, s, c][3]
-            bank = 512 * (2 * s + c)
-            t.wait_ge(sem["hd%d%d" % (s, c)], 1)
-            t.matmul_mx(T.p[:, bank:bank + hn], wq[:, 256:384], ws[:, 256:384], T["hq%d%d" % (s, c)][:, 0:hn],
-                        T["hs%d%d" % (s, c)][:, 0:hn], True, True).then_inc(sem["pd%d%d" % (s, c)], 1)
-
-    A = g.scalar
+    v, A, t = g.vector, g.scalar, g.tensor
     F = ActivationFunctionType
+    hw, tlen = P["hw"][me], P["tlen"][me]
+    xend = P["tl"][me][N + 1]
+    nfeed = engines(core, hcore[me] if role == "A" else cores[me]) // 2
+
+    if role == "A":
+        col, x, nload = 0, off[me][P["s0"][me]], 0
+        while col < tlen:
+            w = min(NC - x, tlen - col)
+            [g.sync, g.scalar][nload % 2].dma_start(T.xt[:, 4 * col:4 * (col + w)], T.x[:, 4 * x:4 * (x + w)]).then_inc(sem.xl, 16)
+            col, x, nload = col + w, 0, nload + 1
+        g.sync.dma_start(T.wt[:, 0:512], T.w1[:, 0:512]).then_inc(sem.wl, 16)
+        g.scalar.dma_start(T.wt[:, 512:1024], T.w1[:, 512:1024]).then_inc(sem.wl, 16)
+        g.sync.dma_start(T.wt[:, 1024:1536], T.w2[:, :]).then_inc(sem.wm, 16)
+        g.scalar.dma_start(T.g1[:, :], T.gt[:, :]).then_inc(sem.gl, 16)
+        v.wait_ge(sem.xl, 16 * nload)
+        v.quantize_mx(T.bq[:, 0:tlen], T.bs[:, 0:tlen], T.xt[:, 0:4 * tlen]).then_inc(sem.xqd, 1)
+        v.wait_ge(sem.wl, 32)
+        v.quantize_mx(T.wq[:, 0:256], T.ws[:, 0:256], T.wt[:, 0:1024]).then_inc(sem.wqd, 1)
+        v.wait_ge(sem.wm, 16)
+        v.quantize_mx(T.wq[:, 256:384], T.ws[:, 256:384], T.wt[:, 1024:1536]).then_inc(sem.wqd, 1)
+        b = bits(topo.mask(core, hcore[me]))
+        masks = [sum(1 << e for e in b[i::2]) for i in range(2)]
+        g.wait_ge(sem.xqd, 1)
+        for f, sm in ((codes, sem.xh), (scales, sem.xhs)):
+            send([(hcore[me], f(0, hw), f(0, hw)), (rcore[me], f(xend - hw, hw), f(xend - hw, hw))], [sm, sm], masks)
+        far = hcore[P["partner"][me]]
+        for i, (a, b, sm) in enumerate(((0, 256, sem.wa), (256, 384, sem.wb))):
+            g.wait_ge(sem.wqd, i + 1)
+            send([(far, T.ws[:, a:b], T.ws[:, a:b])], [sm])
+            send([(far, T.wq[:, a:b].bitcast(u8), T.wq[:, a:b].bitcast(u8))], [sm])
+        g.wait_ge(sem.gl, 16)
+        g.partition_broadcast(T.gb[:, :], T.g1[0:1, :], 128).then_inc(sem.bc, 1)
+    else:
+        for f, sm in ((codes, sem.xh), (scales, sem.xhs)):
+            g.wait_ge(sm, nfeed)
+            for W, ks in P["disp"][me, slot]:
+                send([(unit[k, slot], f(P["xpos"][k, slot][me], W), f(P["src"][me, (k, slot)][0], W)) for k in ks], [sem.xa] * len(ks))
+        if role == "R":
+            g.wait_ge(sem.sent, sent[0])
+            return
+
+    lo, n, sg, hn, loc, cut, p0, p1 = P["work"][u]
+    helper = [rcore, hcore][slot]
+    t.wait_ge(sem.xa, sum(2 * engines(helper[j], core, P["src"][j, u][2]) for j in P["xpos"][u]))
+    if role == "A":
+        t.wait_ge(sem.xqd, 1)
+        t.wait_ge(sem.wqd, 1)
+    else:
+        pc = cores[P["partner"][me]]
+        t.wait_ge(sem.xh, nfeed)
+        t.wait_ge(sem.xhs, nfeed)
+        t.wait_ge(sem.wa, 2 * engines(pc, core))
+    for i in range(2):
+        t.matmul_mx(T.z[:, 512 * i:512 * i + n], T.wq[:, 128 * i:128 * i + 128], T.ws[:, 128 * i:128 * i + 128],
+                    T.bq[:, lo:lo + n], T.bs[:, lo:lo + n], True, True).then_inc([sem.za, sem.zb][i], 1)
+    if role == "A":
+        t.wait_ge(sem.wqd, 2)
+    else:
+        t.wait_ge(sem.wb, 2 * engines(pc, core))
+    t.wait_ge(sem.hd, 1)
+    for i, (a, b) in enumerate(((0, p0), (p1, hn))):
+        t.matmul_mx(T.p[:, 512 * i:512 * i + b - a], T.wq[:, 256:384], T.ws[:, 256:384], T.hq[:, a:b], T.hs[:, a:b],
+                    True, True).then_inc([sem.pd0, sem.pd1][i], 1)
+
+    A.wait_ge(sem.za, 1)
+    for a, m, h in sg:
+        for b, sc in ((0, C), (1, -C)):
+            A.activation(T.h[:, 4 * h + b:4 * (h + m):4], T.z[:, a - lo:a - lo + m], F.Relu, scale=sc).then_inc(sem["as"], 1)
+    v.wait_ge(sem.zb, 1)
+    for a, m, h in sg:
+        z = T.z[:, 512 + a - lo:512 + a - lo + m]
+        v.tensor_scalar(T.h[:, 4 * h + 2:4 * (h + m):4], z, 0.0, C, AluOpType.max, AluOpType.mult).then_inc(sem.av, 1)
+        v.tensor_scalar(T.h[:, 4 * h + 3:4 * (h + m):4], z, -C, 0.0, AluOpType.mult, AluOpType.max).then_inc(sem.av, 1)
+    v.wait_ge(sem.av, 2 * len(sg))
+    v.wait_ge(sem["as"], 2 * len(sg))
+    v.quantize_mx(T.hq[:, 0:hn], T.hs[:, 0:hn], T.h[:, 0:4 * hn]).then_inc(sem.hd, 1)
+
+    v.wait_ge(sem.pd0, 1)
+    A.wait_ge(sem.pd1, 1)
     ncp = {}
+    for i, (W, js) in enumerate(P["order"][u]):
+        for j in js:
+            h, w = loc[j]
+            o = P["opos"][u, j][0]
+            if h < cut:
+                v.tensor_copy(T.out[:, o:o + w], T.p[:, h:h + w]).then_inc(sem["cg%d" % i], 1)
+            else:
+                A.activation(T.out[:, o:o + w], T.p[:, 512 + h - p1:512 + h - p1 + w], F.Copy).then_inc(sem["cg%d" % i], 1)
+            ncp[i] = ncp.get(i, 0) + 1
 
-    def copies(s, c, f):
-        bank = 512 * (2 * s + c)
-        loc = P["work"][me, s, c][4]
-        for i, (jc, j) in enumerate(P["order"][me]):
-            if jc == c and j in loc:
-                h, n = loc[j]
-                o = P["opos"][me, j][0]
-                if s == 1:
-                    a, b = P["pieces"](j, me)[0]
-                    o += b - a
-                f(T.out[:, o:o + n], T.p[:, bank + h:bank + h + n]).then_inc(sem["cg%d" % i], 1)
-                ncp[i] = ncp.get(i, 0) + 1
-
-    for s in range(2):
-        for c in range(2):
-            lo, n, sg, hn, loc = P["work"][me, s, c]
-            ht = T["h%d%d" % (s, c)]
-            A.wait_ge(sem["za%d%d" % (s, c)], 1)
-            bank = 512 * 2 * c - lo
-            for a, m, h in sg:
-                for b, sc in ((0, C), (1, -C)):
-                    A.activation(ht[:, 4 * h + b:4 * (h + m):4], T.z[:, bank + a:bank + a + m], F.Relu, scale=sc).then_inc(sem["as%d%d" % (s, c)], 1)
-            v.wait_ge(sem["zb%d%d" % (s, c)], 1)
-            bank += 512
-            for a, m, h in sg:
-                src = T.z[:, bank + a:bank + a + m]
-                v.tensor_scalar(ht[:, 4 * h + 2:4 * (h + m):4], src, 0.0, C, AluOpType.max, AluOpType.mult).then_inc(sem["av%d%d" % (s, c)], 1)
-                v.tensor_scalar(ht[:, 4 * h + 3:4 * (h + m):4], src, -C, 0.0, AluOpType.mult, AluOpType.max).then_inc(sem["av%d%d" % (s, c)], 1)
-            v.wait_ge(sem["av%d%d" % (s, c)], 2 * len(sg))
-            v.wait_ge(sem["as%d%d" % (s, c)], 2 * len(sg))
-            v.quantize_mx(T["hq%d%d" % (s, c)][:, 0:hn], T["hs%d%d" % (s, c)][:, 0:hn], ht[:, 0:4 * hn]).then_inc(sem["hd%d%d" % (s, c)], 1)
-        A.wait_ge(sem["pd%d0" % s], 1)
-        copies(s, 0, lambda o, i: A.activation(o, i, F.Copy))
-        v.wait_ge(sem["pd%d1" % s], 1)
-        copies(s, 1, lambda o, i: v.tensor_copy(o, i))
-
-    for i, (c, j) in enumerate(P["order"][me]):
+    for i, (W, js) in enumerate(P["order"][u]):
         g.wait_ge(sem["cg%d" % i], ncp[i])
-        o, w, _ = P["opos"][me, j]
-        x = P["rpos"][me, j]
-        send([(j, T.ret[:, x:x + w], T.out[:, o:o + w])], [sem["ra%d" % P["rorder"][j].index(me)]])
+        prs = []
+        for j in js:
+            o, x = P["opos"][u, j][0], P["rpos"][u, j]
+            prs.append((cores[j], T.ret[:, x:x + W], T.out[:, o:o + W]))
+        send(prs, [sem["ra%d" % P["rorder"][j].index(u)] for j in js])
 
-    nm = [0]
+    if role == "A":
+        nm = [0]
 
-    def gate(buf, pos, e):
-        for i, (dst, r) in enumerate(((T.yf, e), (T.ys, (e + 1) % N))):
-            n, o = CNT[me][r], off[me][r]
-            if n:
-                v.tensor_tensor(dst[:, o:o + n], buf[:, pos:pos + n], T.gb[:, NC * i + o:NC * i + o + n], AluOpType.mult).then_inc(sem.mul, 1)
-                nm[0] += 1
-                pos += n
+        def gate(buf, pos, e):
+            for i, (dst, r) in enumerate(((T.yf, e), (T.ys, (e + 1) % N))):
+                w, o = CNT[me][r], off[me][r]
+                if w:
+                    v.tensor_tensor(dst[:, o:o + w], buf[:, pos:pos + w], T.gb[:, NC * i + o:NC * i + o + w], AluOpType.mult).then_inc(sem.mul, 1)
+                    nm[0] += 1
+                    pos += w
 
-    v.wait_ge(sem.bc, 1)
-    for s in range(2):
-        loc = P["work"][me, s, 1][4]
+        v.wait_ge(sem.bc, 1)
         if me in loc:
-            gate(T.p, 512 * (2 * s + 1) + loc[me][0], me if s == 0 else pt)
-    for i, k in enumerate(P["rorder"][me]):
-        x = P["rpos"][k, me]
-        v.wait_ge(sem["ra%d" % i], engines(k, me))
-        a, b = P["pieces"](me, k)[0]
-        gate(T.ret, x, k)
-        gate(T.ret, x + b - a, P["partner"][k])
-    v.wait_ge(sem.mul, nm[0])
-    v.tensor_tensor(T.yb[:, :], T.yf[:, :], T.ys[:, :], AluOpType.add).then_inc(sem.add, 1)
-    g.sync.wait_ge(sem.add, 1)
-    g.sync.dma_start(T.y[:, :], T.yb[:, :]).then_inc(sem.yst, 16)
-    g.sync.wait_ge(sem.yst, 16)
+            gate(T.p, loc[me][0], me)
+        for i, q in enumerate(P["rorder"][me]):
+            v.wait_ge(sem["ra%d" % i], engines(unit[q], core, P["opos"][q, me][4]))
+            gate(T.ret, P["rpos"][q, me], expert[q])
+        v.wait_ge(sem.mul, nm[0])
+        v.tensor_tensor(T.yb[:, :], T.yf[:, :], T.ys[:, :], AluOpType.add).then_inc(sem.add, 1)
+        g.sync.wait_ge(sem.add, 1)
+        g.sync.dma_start(T.y[:, :], T.yb[:, :]).then_inc(sem.yst, 16)
+        g.sync.wait_ge(sem.yst, 16)
     g.wait_ge(sem.sent, sent[0])

@@ -16,9 +16,6 @@ SCRATCH = {
     "ws": ("sbuf", [128, 384], "uint8"),
     "bq": ("sbuf", [128, 1024], "float8_e4m3fn_x4"),
     "bs": ("sbuf", [128, 1024], "uint8"),
-    "h": ("sbuf", [128, 4 * 512], "bfloat16"),
-    "hq": ("sbuf", [128, 512], "float8_e4m3fn_x4"),
-    "hs": ("sbuf", [128, 512], "uint8"),
     "out": ("sbuf", [128, 512], "float32"),
     "ret": ("sbuf", [128, 768], "float32"),
     "g1": ("sbuf", [1, 2 * NC], "bfloat16"),
@@ -26,12 +23,17 @@ SCRATCH = {
     "yf": ("sbuf", [128, NC], "float32"),
     "ys": ("sbuf", [128, NC], "float32"),
     "yb": ("sbuf", [128, NC], "float32"),
-    "z": ("psum", [128, 2 * 512], "float32"),
     "p": ("psum", [128, 2 * 512], "float32"),
+    "po": ("psum", [128, 512], "float32"),
 }
-
-SEMAPHORES = ["xl", "wl", "wm", "gl", "xqd", "wqd", "xh", "xhs", "xa", "wa", "wb", "za", "zb", "as", "av", "hd",
-              "pd0", "pd1", "sent", "bc", "mul", "add", "yst"]
+SEMAPHORES = ["xl", "wl0", "wl1", "wl2", "gl", "xqd", "wqd", "xh", "xhs", "xa", "wa", "wx", "wb", "wr", "pd0", "pd1", "pdo",
+              "sent", "bc", "mul", "add", "yst"]
+for _c in "mo":
+    SCRATCH["h" + _c] = ("sbuf", [128, 4 * 512], "bfloat16")
+    SCRATCH["hq" + _c] = ("sbuf", [128, 512], "float8_e4m3fn_x4")
+    SCRATCH["hs" + _c] = ("sbuf", [128, 512], "uint8")
+    SCRATCH["z" + _c] = ("psum", [128, 2 * 512], "float32")
+    SEMAPHORES += [_n + _c for _n in ("za", "zb", "as", "av", "hd")]
 for _i in range(12):
     SEMAPHORES += ["cg%d" % _i, "ra%d" % _i]
 
@@ -79,12 +81,15 @@ def make_plan(T, topo):
     partner = [[q for q in range(N) if rack[q] != rack[r] and topo.chip(cores[q]) == topo.chip(cores[r])
                 and topo.may_write(cores[r], cores[q])][0] for r in range(N)]
     peers = [[q for q in range(N) if rack[q] == rack[r] and q != r] for r in range(N)]
-    hcore, rcore = [], []
+    hcore, rcore, wcore = [], [], []
     for r in range(N):
-        ok = [c for c in range(CORES_ALL) if topo.host(c) == topo.host(cores[r]) and topo.chip(c) == topo.chip(cores[r])
-              and c != cores[r] and all(topo.may_write(c, cores[q]) for q in peers[r])]
-        hcore.append([c for c in ok if topo.die(c) != topo.die(cores[r])][0])
-        rcore.append([c for c in ok if topo.die(c) == topo.die(cores[r])][0])
+        chip = [c for c in range(CORES_ALL) if topo.host(c) == topo.host(cores[r]) and topo.chip(c) == topo.chip(cores[r])
+                and c != cores[r]]
+        free = [c for c in chip if all(topo.may_write(c, cores[q]) for q in peers[r])]
+        rest = [c for c in chip if c not in free and topo.may_write(c, cores[partner[r]])]
+        hcore.append([c for c in free if topo.die(c) != topo.die(cores[r])][0])
+        rcore.append([c for c in free if topo.die(c) == topo.die(cores[r])][0])
+        wcore.append([[c for c in rest if topo.die(c) == topo.die(cores[r])][0], [c for c in rest if topo.die(c) != topo.die(cores[r])][0]])
     unit = {}
     for r in range(N):
         unit[r, 0], unit[r, 1] = cores[r], hcore[r]
@@ -124,15 +129,19 @@ def make_plan(T, topo):
                 lst.append((W, [k for _, k in q]))
             disp[j, s] = lst
 
-    xpos, work = {}, {}
+    xpos, work, ownwork = {}, {}, {}
     for k in range(N):
+        a, b = win(k, (k, 0))
+        n = max(MINW, b - a)
+        lo = max(0, b - n)
+        ownwork[k] = (lo, n, [(lo, n, 0)], n, a - lo, b - a)
         for s in range(2):
             u = (k, s)
             base = tlen[k] if s == 0 else hw[k]
             best = None
             for q in perms([j for j in peers[k] if (j, u) in src]):
                 x, pos, ps = base, {}, []
-                if width(k, u):
+                if s == 1 and width(k, u):
                     ps.append((win(k, u)[0], width(k, u), k))
                 for j in q:
                     pos[j] = x
@@ -205,9 +214,10 @@ def make_plan(T, topo):
     role = {}
     for r in range(N):
         role[cores[r]], role[hcore[r]], role[rcore[r]] = (r, "A"), (r, "H"), (r, "R")
-    P = {"N": N, "cores": cores, "off": off, "partner": partner, "hcore": hcore, "rcore": rcore, "unit": unit,
+        role[wcore[r][0]], role[wcore[r][1]] = (r, "W1"), (r, "W2")
+    P = {"N": N, "cores": cores, "off": off, "partner": partner, "hcore": hcore, "rcore": rcore, "wcore": wcore, "unit": unit,
          "expert": expert, "s0": s0, "tl": tl, "tlen": tlen, "hw": hw, "disp": disp, "src": src, "xpos": xpos, "work": work,
-         "order": order, "opos": opos, "rpos": rpos, "rorder": rorder, "cnt": CNT, "role": role}
+         "ownwork": ownwork, "order": order, "opos": opos, "rpos": rpos, "rorder": rorder, "cnt": CNT, "role": role}
     _cache["plan"] = P
     return P
 
@@ -218,12 +228,14 @@ def rank_program(g, core, T, topo):
         return
     me, role = P["role"][core]
     N, cores, CNT, off = P["N"], P["cores"], P["cnt"], P["off"]
-    unit, expert, hcore, rcore = P["unit"], P["expert"], P["hcore"], P["rcore"]
+    unit, expert, hcore, rcore, wcore = P["unit"], P["expert"], P["hcore"], P["rcore"], P["wcore"]
     sem = T.sem
     u8 = dt.uint8
     sent = [0]
     slot = 1 if role == "H" else 0
     u = (me, slot)
+    pt = P["partner"][me]
+    far = hcore[pt]
 
     def send(pairs, remote, masks=None):
         n = len(pairs)
@@ -242,11 +254,24 @@ def rank_program(g, core, T, topo):
     def engines(a, b, n=1):
         return len(bits(topo.mask(a, b))) // n
 
+    def inside(a, b, c):
+        return topo.mask(a, b) & ~topo.mask(a, c)
+
     def codes(x, w):
         return T.bq[:, x:x + w].bitcast(u8)
 
     def scales(x, w):
         return T.bs[:, x:x + w]
+
+    def wcodes(i):
+        return T.wq[:, 128 * i:128 * i + 128].bitcast(u8)
+
+    if role in ("W1", "W2"):
+        i = 1 if role == "W1" else 2
+        g.wait_ge(sem.wr, len(bits(inside(cores[me], core, far))))
+        send([(far, wcodes(i), wcodes(i))], [sem.wx if i == 1 else sem.wb])
+        g.wait_ge(sem.sent, sent[0])
+        return
 
     v, A, t = g.vector, g.scalar, g.tensor
     F = ActivationFunctionType
@@ -254,34 +279,69 @@ def rank_program(g, core, T, topo):
     xend = P["tl"][me][N + 1]
     nfeed = engines(core, hcore[me] if role == "A" else cores[me]) // 2
 
+    def products(c, lo, n, i):
+        z = T["z" + c]
+        t.matmul_mx(z[:, 512 * i:512 * i + n], T.wq[:, 128 * i:128 * i + 128], T.ws[:, 128 * i:128 * i + 128],
+                    T.bq[:, lo:lo + n], T.bs[:, lo:lo + n], True, True).then_inc(sem[("za", "zb")[i] + c], 1)
+
+    def second(c, p, a, b, sm):
+        t.matmul_mx(p, T.wq[:, 256:384], T.ws[:, 256:384], T["hq" + c][:, a:b], T["hs" + c][:, a:b], True, True).then_inc(sm, 1)
+
+    def steps(c, lo, sg, hn):
+        z, h = T["z" + c], T["h" + c]
+        A.wait_ge(sem["za" + c], 1)
+        for a, m, x in sg:
+            for b, sc in ((0, C), (1, -C)):
+                A.activation(h[:, 4 * x + b:4 * (x + m):4], z[:, a - lo:a - lo + m], F.Relu, scale=sc).then_inc(sem["as" + c], 1)
+        v.wait_ge(sem["zb" + c], 1)
+        for a, m, x in sg:
+            zi = z[:, 512 + a - lo:512 + a - lo + m]
+            v.tensor_scalar(h[:, 4 * x + 2:4 * (x + m):4], zi, 0.0, C, AluOpType.max, AluOpType.mult).then_inc(sem["av" + c], 1)
+            v.tensor_scalar(h[:, 4 * x + 3:4 * (x + m):4], zi, -C, 0.0, AluOpType.mult, AluOpType.max).then_inc(sem["av" + c], 1)
+        v.wait_ge(sem["av" + c], 2 * len(sg))
+        v.wait_ge(sem["as" + c], 2 * len(sg))
+        v.quantize_mx(T["hq" + c][:, 0:hn], T["hs" + c][:, 0:hn], h[:, 0:4 * hn]).then_inc(sem["hd" + c], 1)
+
     if role == "A":
         col, x, nload = 0, off[me][P["s0"][me]], 0
         while col < tlen:
             w = min(NC - x, tlen - col)
             [g.sync, g.scalar][nload % 2].dma_start(T.xt[:, 4 * col:4 * (col + w)], T.x[:, 4 * x:4 * (x + w)]).then_inc(sem.xl, 16)
             col, x, nload = col + w, 0, nload + 1
-        g.sync.dma_start(T.wt[:, 0:512], T.w1[:, 0:512]).then_inc(sem.wl, 16)
-        g.scalar.dma_start(T.wt[:, 512:1024], T.w1[:, 512:1024]).then_inc(sem.wl, 16)
-        g.sync.dma_start(T.wt[:, 1024:1536], T.w2[:, :]).then_inc(sem.wm, 16)
+        g.sync.dma_start(T.wt[:, 512:1024], T.w1[:, 512:1024]).then_inc(sem.wl1, 16)
+        g.scalar.dma_start(T.wt[:, 0:512], T.w1[:, 0:512]).then_inc(sem.wl0, 16)
+        g.sync.dma_start(T.wt[:, 1024:1536], T.w2[:, :]).then_inc(sem.wl2, 16)
         g.scalar.dma_start(T.g1[:, :], T.gt[:, :]).then_inc(sem.gl, 16)
         v.wait_ge(sem.xl, 16 * nload)
         v.quantize_mx(T.bq[:, 0:tlen], T.bs[:, 0:tlen], T.xt[:, 0:4 * tlen]).then_inc(sem.xqd, 1)
-        v.wait_ge(sem.wl, 32)
-        v.quantize_mx(T.wq[:, 0:256], T.ws[:, 0:256], T.wt[:, 0:1024]).then_inc(sem.wqd, 1)
-        v.wait_ge(sem.wm, 16)
-        v.quantize_mx(T.wq[:, 256:384], T.ws[:, 256:384], T.wt[:, 1024:1536]).then_inc(sem.wqd, 1)
+        for i in (1, 0, 2):
+            v.wait_ge(sem["wl%d" % i], 16)
+            v.quantize_mx(T.wq[:, 128 * i:128 * i + 128], T.ws[:, 128 * i:128 * i + 128], T.wt[:, 512 * i:512 * i + 512]).then_inc(sem.wqd, 1)
         b = bits(topo.mask(core, hcore[me]))
         masks = [sum(1 << e for e in b[i::2]) for i in range(2)]
         g.wait_ge(sem.xqd, 1)
         for f, sm in ((codes, sem.xh), (scales, sem.xhs)):
             send([(hcore[me], f(0, hw), f(0, hw)), (rcore[me], f(xend - hw, hw), f(xend - hw, hw))], [sm, sm], masks)
-        far = hcore[P["partner"][me]]
-        for i, (a, b, sm) in enumerate(((0, 256, sem.wa), (256, 384, sem.wb))):
-            g.wait_ge(sem.wqd, i + 1)
-            send([(far, T.ws[:, a:b], T.ws[:, a:b])], [sm])
-            send([(far, T.wq[:, a:b].bitcast(u8), T.wq[:, a:b].bitcast(u8))], [sm])
+        wm = [inside(core, c, far) for c in wcore[me]]
+        g.wait_ge(sem.wqd, 1)
+        send([(wcore[me][0], wcodes(1), wcodes(1))], [sem.wr], wm[0:1])
+        g.wait_ge(sem.wqd, 2)
+        send([(far, T.ws[:, 0:256], T.ws[:, 0:256])], [sem.wa])
+        send([(far, wcodes(0), wcodes(0))], [sem.wa])
+        g.wait_ge(sem.wqd, 3)
+        send([(wcore[me][1], wcodes(2), wcodes(2))], [sem.wr], wm[1:2])
+        send([(far, T.ws[:, 256:384], T.ws[:, 256:384])], [sem.wb])
         g.wait_ge(sem.gl, 16)
         g.partition_broadcast(T.gb[:, :], T.g1[0:1, :], 128).then_inc(sem.bc, 1)
+        olo, on, osg, ohn, oloc, ow = P["ownwork"][me]
+        t.wait_ge(sem.xqd, 1)
+        t.wait_ge(sem.wqd, 2)
+        for i in range(2):
+            products("o", olo, on, i)
+        t.wait_ge(sem.wqd, 3)
+        t.wait_ge(sem.hdo, 1)
+        second("o", T.po[:, 0:ohn], 0, ohn, sem.pdo)
+        steps("o", olo, osg, ohn)
     else:
         for f, sm in ((codes, sem.xh), (scales, sem.xhs)):
             g.wait_ge(sm, nfeed)
@@ -294,38 +354,20 @@ def rank_program(g, core, T, topo):
     lo, n, sg, hn, loc, cut, p0, p1 = P["work"][u]
     helper = [rcore, hcore][slot]
     t.wait_ge(sem.xa, sum(2 * engines(helper[j], core, P["src"][j, u][2]) for j in P["xpos"][u]))
-    if role == "A":
-        t.wait_ge(sem.xqd, 1)
-        t.wait_ge(sem.wqd, 1)
-    else:
-        pc = cores[P["partner"][me]]
+    if role == "H":
         t.wait_ge(sem.xh, nfeed)
         t.wait_ge(sem.xhs, nfeed)
-        t.wait_ge(sem.wa, 2 * engines(pc, core))
-    for i in range(2):
-        t.matmul_mx(T.z[:, 512 * i:512 * i + n], T.wq[:, 128 * i:128 * i + 128], T.ws[:, 128 * i:128 * i + 128],
-                    T.bq[:, lo:lo + n], T.bs[:, lo:lo + n], True, True).then_inc([sem.za, sem.zb][i], 1)
-    if role == "A":
-        t.wait_ge(sem.wqd, 2)
-    else:
-        t.wait_ge(sem.wb, 2 * engines(pc, core))
-    t.wait_ge(sem.hd, 1)
-    for i, (a, b) in enumerate(((0, p0), (p1, hn))):
-        t.matmul_mx(T.p[:, 512 * i:512 * i + b - a], T.wq[:, 256:384], T.ws[:, 256:384], T.hq[:, a:b], T.hs[:, a:b],
-                    True, True).then_inc([sem.pd0, sem.pd1][i], 1)
-
-    A.wait_ge(sem.za, 1)
-    for a, m, h in sg:
-        for b, sc in ((0, C), (1, -C)):
-            A.activation(T.h[:, 4 * h + b:4 * (h + m):4], T.z[:, a - lo:a - lo + m], F.Relu, scale=sc).then_inc(sem["as"], 1)
-    v.wait_ge(sem.zb, 1)
-    for a, m, h in sg:
-        z = T.z[:, 512 + a - lo:512 + a - lo + m]
-        v.tensor_scalar(T.h[:, 4 * h + 2:4 * (h + m):4], z, 0.0, C, AluOpType.max, AluOpType.mult).then_inc(sem.av, 1)
-        v.tensor_scalar(T.h[:, 4 * h + 3:4 * (h + m):4], z, -C, 0.0, AluOpType.mult, AluOpType.max).then_inc(sem.av, 1)
-    v.wait_ge(sem.av, 2 * len(sg))
-    v.wait_ge(sem["as"], 2 * len(sg))
-    v.quantize_mx(T.hq[:, 0:hn], T.hs[:, 0:hn], T.h[:, 0:4 * hn]).then_inc(sem.hd, 1)
+        t.wait_ge(sem.wa, 2 * engines(cores[pt], core))
+    products("m", lo, n, 0)
+    if role == "H":
+        t.wait_ge(sem.wx, engines(wcore[pt][0], core))
+    products("m", lo, n, 1)
+    if role == "H":
+        t.wait_ge(sem.wb, engines(wcore[pt][1], core) + engines(cores[pt], core))
+    t.wait_ge(sem.hdm, 1)
+    second("m", T.p[:, 0:p0], 0, p0, sem.pd0)
+    second("m", T.p[:, 512:512 + hn - p1], p1, hn, sem.pd1)
+    steps("m", lo, sg, hn)
 
     v.wait_ge(sem.pd0, 1)
     A.wait_ge(sem.pd1, 1)
@@ -360,8 +402,8 @@ def rank_program(g, core, T, topo):
                     pos += w
 
         v.wait_ge(sem.bc, 1)
-        if me in loc:
-            gate(T.p, loc[me][0], me)
+        v.wait_ge(sem.pdo, 1)
+        gate(T.po, oloc, me)
         for i, q in enumerate(P["rorder"][me]):
             v.wait_ge(sem["ra%d" % i], engines(unit[q], core, P["opos"][q, me][4]))
             gate(T.ret, P["rpos"][q, me], expert[q])

import numpy as np
from concourse.bass import DstId, RemoteDMATransfer
from concourse.mybir import dt, AluOpType, ActivationFunctionType

NC = 192
C = float(np.float32(0.041))
MINW = 128
GAP = 48
CORES_ALL = 512
PADMAX = 36

SCRATCH = {
    "xt": ("sbuf", [128, 4 * 288], "bfloat16"),
    "wt": ("sbuf", [128, 1536], "bfloat16"),
    "wq": ("sbuf", [128, 384], "float8_e4m3fn_x4"),
    "ws": ("sbuf", [128, 384], "uint8"),
    "bq": ("sbuf", [128, 1024], "float8_e4m3fn_x4"),
    "bs": ("sbuf", [128, 1024], "uint8"),
    "out": ("sbuf", [128, 512], "float32"),
    "ret": ("sbuf", [128, 768], "float32"),
    "g1": ("sbuf", [1, 2 * NC], "bfloat16"),
    "gb": ("sbuf", [128, 2 * NC], "bfloat16"),
    "yf": ("sbuf", [128, NC], "float32"),
    "ys": ("sbuf", [128, NC], "float32"),
    "yb": ("sbuf", [128, NC], "float32"),
    "p": ("psum", [128, 2 * 512], "float32"),
    "po": ("psum", [128, 512], "float32"),
}
SEMAPHORES = ["xl", "wl0", "wl1", "wl2", "gl", "xqd", "wqd", "xh", "xhs", "xa", "wa", "wx", "wb", "wr", "pd0", "pd1", "pdo",
              "sent", "bc", "mul", "add", "yst"]
for _c in "mo":
    SCRATCH["h" + _c] = ("sbuf", [128, 4 * 512], "bfloat16")
    SCRATCH["hq" + _c] = ("sbuf", [128, 512], "float8_e4m3fn_x4")
    SCRATCH["hs" + _c] = ("sbuf", [128, 512], "uint8")
    SCRATCH["z" + _c] = ("psum", [128, 2 * 512], "float32")
    SEMAPHORES += [_n + _c for _n in ("za", "zb", "as", "av", "hd")]
for _i in range(12):
    SEMAPHORES += ["cg%d" % _i, "ra%d" % _i]

_cache = {}


def bits(m):
    return [i for i in range(16) if (m >> i) & 1]


def share(m, n):
    b = bits(m)
    k = len(b) // n
    return [sum(1 << e for e in b[k * i:k * i + k]) for i in range(n)]


def perms(q):
    return [[q[i]] + r for i in range(len(q)) for r in perms(q[:i] + q[i + 1:])] if q else [[]]


def splits(items, sizes):
    if not items:
        return [[]]
    res, a, rest = [], items[0], items[1:]

    def choose(q, n):
        if n == 0:
            return [[]]
        return [[q[i]] + r for i in range(len(q)) for r in choose(q[i + 1:], n - 1)]

    for n in sizes:
        for c in choose(rest, n - 1):
            res += [[[a] + c] + r for r in splits([x for x in rest if x not in c], sizes)]
    return res


def make_plan(T, topo):
    if "plan" in _cache:
        return _cache["plan"]
    CNT = T.tables["CNT"]
    cores = list(T.cores)
    N = len(cores)
    off = [[sum(c[:e]) for e in range(N + 1)] for c in CNT]
    rack = [topo.rack(topo.host(c)) for c in cores]
    partner = [[q for q in range(N) if rack[q] != rack[r] and topo.chip(cores[q]) == topo.chip(cores[r])
                and topo.may_write(cores[r], cores[q])][0] for r in range(N)]
    peers = [[q for q in range(N) if rack[q] == rack[r] and q != r] for r in range(N)]
    hcore, rcore, wcore = [], [], []
    for r in range(N):
        chip = [c for c in range(CORES_ALL) if topo.host(c) == topo.host(cores[r]) and topo.chip(c) == topo.chip(cores[r])
                and c != cores[r]]
        free = [c for c in chip if all(topo.may_write(c, cores[q]) for q in peers[r])]
        rest = [c for c in chip if c not in free and topo.may_write(c, cores[partner[r]])]
        hcore.append([c for c in free if topo.die(c) != topo.die(cores[r])][0])
        rcore.append([c for c in free if topo.die(c) == topo.die(cores[r])][0])
        wcore.append([[c for c in rest if topo.die(c) == topo.die(cores[r])][0], [c for c in rest if topo.die(c) != topo.die(cores[r])][0]])
    unit = {}
    for r in range(N):
        unit[r, 0], unit[r, 1] = cores[r], hcore[r]
    expert = {(r, s): (r, partner[r])[s] for r in range(N) for s in range(2)}
    half = N // 2
    s0 = [min(partner[q] for q in range(N) if rack[q] == rack[j]) for j in range(N)]
    tl = [[sum(CNT[j][(s0[j] + k) % N] for k in range(i)) for i in range(N + 2)] for j in range(N)]
    tlen = [(tl[j][N + 1] + 15) // 16 * 16 for j in range(N)]
    hw = [max(MINW, tl[j][half + 1], tl[j][N + 1] - tl[j][half]) for j in range(N)]

    def win(j, u):
        i = (expert[u] - s0[j]) % N
        return tl[j][i], tl[j][i + 2]

    def width(j, u):
        a, b = win(j, u)
        return b - a

    CALL, ROW, BYTE = 300.0, 20.0, 1 / 15.0

    disp, src = {}, {}
    for j in range(N):
        for s in range(2):
            items = [(width(j, (k, s)), k) for k in peers[j] if width(j, (k, s))]

            def cost(gs):
                return sum(2 * CALL + 16 * len(q) * (2 * ROW + 5 * BYTE * max(q)[0]) for q in gs)

            gs = min(splits(items, (1, 2, 4)), key=cost)
            gs.sort(key=lambda q: (-len(q), -max(q)[0]))
            end = hw[j] if s == 1 else tl[j][N + 1]
            lst = []
            for q in gs:
                W = max(q)[0]
                for _, k in q:
                    src[j, (k, s)] = (min(win(j, (k, s))[0], end - W), W, len(q))
                lst.append((W, [k for _, k in q]))
            disp[j, s] = lst

    xpos, work, ownwork = {}, {}, {}
    for k in range(N):
        a, b = win(k, (k, 0))
        n = max(MINW, b - a)
        lo = max(0, b - n)
        ownwork[k] = (lo, n, [(lo, n, 0)], n, a - lo, b - a)
        for s in range(2):
            u = (k, s)
            base = tlen[k] if s == 0 else hw[k]
            best = None
            for q in perms([j for j in peers[k] if (j, u) in src]):
                x, pos, ps = base, {}, []
                if s == 1 and width(k, u):
                    ps.append((win(k, u)[0], width(k, u), k))
                for j in q:
                    pos[j] = x
                    ps.append((x + win(j, u)[0] - src[j, u][0], width(j, u), j))
                    x += src[j, u][1]
                lo, hi = ps[0][0], ps[-1][0] + ps[-1][1]
                segs = [[a, a + w] for a, w, _ in ps]
                while len(segs) > 1:
                    gap, i = min((segs[i + 1][0] - segs[i][1], i) for i in range(len(segs) - 1))
                    if gap >= GAP and sum(b - a for a, b in segs) + gap > MINW:
                        break
                    segs[i:i + 2] = [[segs[i][0], segs[i + 1][1]]]
                need = MINW - sum(b - a for a, b in segs)
                for i in range(len(segs) - 1):
                    if need > 0:
                        d = min(need, segs[i + 1][0] - segs[i][1])
                        segs[i][1] += d
                        need -= d
                if need > 0:
                    segs[0][0] -= need
                lo = min(lo, segs[0][0], hi - MINW)
                hn, sg = 0, []
                for a, b in segs:
                    sg.append((a, b - a, hn))
                    hn += b - a
                c = 1.7 * (hi - lo) + 2.6 * hn + 110 * len(sg)
                if best is None or c < best[0]:
                    loc = {}
                    for x1, w, j in ps:
                        for a, n, h in sg:
                            if a <= x1 and x1 + w <= a + n:
                                loc[j] = (h + x1 - a, w)
                    best = (c, pos, (lo, hi - lo, sg, hn, loc))
            xpos[u], w = best[1], best[2]
            hn, loc = w[3], w[4]
            cut = min([h for h, _ in loc.values()] + [hn], key=lambda b: abs(2 * b - hn))
            work[u] = w + (cut, max(cut, MINW), min(cut, hn - MINW))
    order, opos = {}, {}
    for k in range(N):
        for s in range(2):
            u = (k, s)
            items = [(width(j, u), j) for j in peers[k] if width(j, u)]
            cand = []
            for gs in splits(items, (1, 2)):
                pad = sum(max(q)[0] - w for q in gs for w, _ in q)
                if pad <= PADMAX:
                    cand.append((sum(CALL + 16 * len(q) * (ROW + 4 * BYTE * max(q)[0]) for q in gs), gs))
            gs = min(cand, key=lambda c: c[0])[1]
            gs.sort(key=lambda q: -max(q)[0])
            if s == 1 and width(k, u):
                gs.append([(width(k, u), k)])
            o, lst = 0, []
            for i, q in enumerate(gs):
                q.sort()
                W = max(q)[0]
                for w, j in q:
                    opos[u, j] = (o, w, W, i, len(q))
                    o += w
                lst.append((W, [j for _, j in q]))
            order[u] = lst
    rpos, rorder = {}, []
    for j in range(N):
        us = [(k, s) for k in range(N) for s in range(2) if ((k, s), j) in opos]
        us.sort(key=lambda u: (opos[u, j][3], u[1], u[0]))
        x = 0
        for u in us:
            rpos[u, j] = x
            x += opos[u, j][2]
        rorder.append(us)
    role = {}
    for r in range(N):
        role[cores[r]], role[hcore[r]], role[rcore[r]] = (r, "A"), (r, "H"), (r, "R")
        role[wcore[r][0]], role[wcore[r][1]] = (r, "W1"), (r, "W2")
    P = {"N": N, "cores": cores, "off": off, "partner": partner, "hcore": hcore, "rcore": rcore, "wcore": wcore, "unit": unit,
         "expert": expert, "s0": s0, "tl": tl, "tlen": tlen, "hw": hw, "disp": disp, "src": src, "xpos": xpos, "work": work,
         "ownwork": ownwork, "order": order, "opos": opos, "rpos": rpos, "rorder": rorder, "cnt": CNT, "role": role}
    _cache["plan"] = P
    return P


def rank_program(g, core, T, topo):
    P = make_plan(T, topo)
    if core not in P["role"]:
        return
    me, role = P["role"][core]
    N, cores, CNT, off = P["N"], P["cores"], P["cnt"], P["off"]
    unit, expert, hcore, rcore, wcore = P["unit"], P["expert"], P["hcore"], P["rcore"], P["wcore"]
    sem = T.sem
    u8 = dt.uint8
    sent = [0]
    slot = 1 if role == "H" else 0
    u = (me, slot)
    pt = P["partner"][me]
    far = hcore[pt]

    def send(pairs, remote, masks=None):
        n = len(pairs)
        trs = []
        for i, (d, o, a) in enumerate(pairs):
            m = masks[i] if masks else share(topo.mask(core, d), n)[i]
            rid, pid = topo.addr(d, core)
            if n == 1:
                g.remote_dma(o, a, remote[i], sem.sent, pid, rid, m)
            else:
                trs.append(RemoteDMATransfer(dst_ids=[DstId(rid=rid, pnc=pid)], dma_engine_mask=m, remote_sem=remote[i], src=a, dst=o))
            sent[0] += len(bits(m))
        if trs:
            g.remote_dma_fused(trs, local_sem=sem.sent)

    def engines(a, b, n=1):
        return len(bits(topo.mask(a, b))) // n

    def inside(a, b, c):
        return topo.mask(a, b) & ~topo.mask(a, c)

    def codes(x, w):
        return T.bq[:, x:x + w].bitcast(u8)

    def scales(x, w):
        return T.bs[:, x:x + w]

    def wcodes(i):
        return T.wq[:, 128 * i:128 * i + 128].bitcast(u8)

    if role in ("W1", "W2"):
        i = 1 if role == "W1" else 2
        g.wait_ge(sem.wr, len(bits(inside(cores[me], core, far))))
        send([(far, wcodes(i), wcodes(i))], [sem.wx if i == 1 else sem.wb])
        g.wait_ge(sem.sent, sent[0])
        return

    v, A, t = g.vector, g.scalar, g.tensor
    F = ActivationFunctionType
    hw, tlen = P["hw"][me], P["tlen"][me]
    xend = P["tl"][me][N + 1]
    nfeed = engines(core, hcore[me] if role == "A" else cores[me]) // 2

    def products(c, lo, n, i):
        z = T["z" + c]
        t.matmul_mx(z[:, 512 * i:512 * i + n], T.wq[:, 128 * i:128 * i + 128], T.ws[:, 128 * i:128 * i + 128],
                    T.bq[:, lo:lo + n], T.bs[:, lo:lo + n], True, True).then_inc(sem[("za", "zb")[i] + c], 1)

    def second(c, p, a, b, sm):
        t.matmul_mx(p, T.wq[:, 256:384], T.ws[:, 256:384], T["hq" + c][:, a:b], T["hs" + c][:, a:b], True, True).then_inc(sm, 1)

    def steps(c, lo, sg, hn):
        z, h = T["z" + c], T["h" + c]
        A.wait_ge(sem["za" + c], 1)
        for a, m, x in sg:
            for b, sc in ((0, C), (1, -C)):
                A.activation(h[:, 4 * x + b:4 * (x + m):4], z[:, a - lo:a - lo + m], F.Relu, scale=sc).then_inc(sem["as" + c], 1)
        v.wait_ge(sem["zb" + c], 1)
        for a, m, x in sg:
            zi = z[:, 512 + a - lo:512 + a - lo + m]
            v.tensor_scalar(h[:, 4 * x + 2:4 * (x + m):4], zi, 0.0, C, AluOpType.max, AluOpType.mult).then_inc(sem["av" + c], 1)
            v.tensor_scalar(h[:, 4 * x + 3:4 * (x + m):4], zi, -C, 0.0, AluOpType.mult, AluOpType.max).then_inc(sem["av" + c], 1)
        v.wait_ge(sem["av" + c], 2 * len(sg))
        v.wait_ge(sem["as" + c], 2 * len(sg))
        v.quantize_mx(T["hq" + c][:, 0:hn], T["hs" + c][:, 0:hn], h[:, 0:4 * hn]).then_inc(sem["hd" + c], 1)

    if role == "A":
        col, x, nload = 0, off[me][P["s0"][me]], 0
        while col < tlen:
            w = min(NC - x, tlen - col)
            [g.sync, g.scalar][nload % 2].dma_start(T.xt[:, 4 * col:4 * (col + w)], T.x[:, 4 * x:4 * (x + w)]).then_inc(sem.xl, 16)
            col, x, nload = col + w, 0, nload + 1
        g.sync.dma_start(T.wt[:, 512:1024], T.w1[:, 512:1024]).then_inc(sem.wl1, 16)
        g.scalar.dma_start(T.wt[:, 0:512], T.w1[:, 0:512]).then_inc(sem.wl0, 16)
        g.sync.dma_start(T.wt[:, 1024:1536], T.w2[:, :]).then_inc(sem.wl2, 16)
        g.scalar.dma_start(T.g1[:, :], T.gt[:, :]).then_inc(sem.gl, 16)
        v.wait_ge(sem.xl, 16 * nload)
        v.quantize_mx(T.bq[:, 0:tlen], T.bs[:, 0:tlen], T.xt[:, 0:4 * tlen]).then_inc(sem.xqd, 1)
        for i in (1, 0, 2):
            v.wait_ge(sem["wl%d" % i], 16)
            v.quantize_mx(T.wq[:, 128 * i:128 * i + 128], T.ws[:, 128 * i:128 * i + 128], T.wt[:, 512 * i:512 * i + 512]).then_inc(sem.wqd, 1)
        b = bits(topo.mask(core, hcore[me]))
        masks = [sum(1 << e for e in b[i::2]) for i in range(2)]
        g.wait_ge(sem.xqd, 1)
        for f, sm in ((codes, sem.xh), (scales, sem.xhs)):
            send([(hcore[me], f(0, hw), f(0, hw)), (rcore[me], f(xend - hw, hw), f(xend - hw, hw))], [sm, sm], masks)
        wm = [inside(core, c, far) for c in wcore[me]]
        g.wait_ge(sem.wqd, 1)
        send([(wcore[me][0], wcodes(1), wcodes(1))], [sem.wr], wm[0:1])
        g.wait_ge(sem.wqd, 2)
        send([(far, T.ws[:, 0:256], T.ws[:, 0:256])], [sem.wa])
        send([(far, wcodes(0), wcodes(0))], [sem.wa])
        g.wait_ge(sem.wqd, 3)
        send([(wcore[me][1], wcodes(2), wcodes(2))], [sem.wr], wm[1:2])
        send([(far, T.ws[:, 256:384], T.ws[:, 256:384])], [sem.wb])
        g.wait_ge(sem.gl, 16)
        g.partition_broadcast(T.gb[:, :], T.g1[0:1, :], 128).then_inc(sem.bc, 1)
        olo, on, osg, ohn, oloc, ow = P["ownwork"][me]
        t.wait_ge(sem.xqd, 1)
        t.wait_ge(sem.wqd, 2)
        for i in range(2):
            products("o", olo, on, i)
        t.wait_ge(sem.wqd, 3)
        t.wait_ge(sem.hdo, 1)
        second("o", T.po[:, 0:ohn], 0, ohn, sem.pdo)
        steps("o", olo, osg, ohn)
    else:
        for f, sm in ((codes, sem.xh), (scales, sem.xhs)):
            g.wait_ge(sm, nfeed)
            for W, ks in P["disp"][me, slot]:
                send([(unit[k, slot], f(P["xpos"][k, slot][me], W), f(P["src"][me, (k, slot)][0], W)) for k in ks], [sem.xa] * len(ks))
        if role == "R":
            g.wait_ge(sem.sent, sent[0])
            return

    lo, n, sg, hn, loc, cut, p0, p1 = P["work"][u]
    helper = [rcore, hcore][slot]
    t.wait_ge(sem.xa, sum(2 * engines(helper[j], core, P["src"][j, u][2]) for j in P["xpos"][u]))
    if role == "H":
        t.wait_ge(sem.xh, nfeed)
        t.wait_ge(sem.xhs, nfeed)
        t.wait_ge(sem.wa, 2 * engines(cores[pt], core))
    products("m", lo, n, 0)
    if role == "H":
        t.wait_ge(sem.wx, engines(wcore[pt][0], core))
    products("m", lo, n, 1)
    if role == "H":
        t.wait_ge(sem.wb, engines(wcore[pt][1], core) + engines(cores[pt], core))
    t.wait_ge(sem.hdm, 1)
    second("m", T.p[:, 0:p0], 0, p0, sem.pd0)
    second("m", T.p[:, 512:512 + hn - p1], p1, hn, sem.pd1)
    steps("m", lo, sg, hn)

    v.wait_ge(sem.pd0, 1)
    A.wait_ge(sem.pd1, 1)
    ncp = {}
    for i, (W, js) in enumerate(P["order"][u]):
        for j in js:
            h, w = loc[j]
            o = P["opos"][u, j][0]
            if h < cut:
                v.tensor_copy(T.out[:, o:o + w], T.p[:, h:h + w]).then_inc(sem["cg%d" % i], 1)
            else:
                A.activation(T.out[:, o:o + w], T.p[:, 512 + h - p1:512 + h - p1 + w], F.Copy).then_inc(sem["cg%d" % i], 1)
            ncp[i] = ncp.get(i, 0) + 1

    for i, (W, js) in enumerate(P["order"][u]):
        g.wait_ge(sem["cg%d" % i], ncp[i])
        prs = []
        for j in js:
            o, x = P["opos"][u, j][0], P["rpos"][u, j]
            prs.append((cores[j], T.ret[:, x:x + W], T.out[:, o:o + W]))
        send(prs, [sem["ra%d" % P["rorder"][j].index(u)] for j in js])

    if role == "A":
        nm = [0]

        def gate(buf, pos, e):
            for i, (dst, r) in enumerate(((T.yf, e), (T.ys, (e + 1) % N))):
                w, o = CNT[me][r], off[me][r]
                if w:
                    v.tensor_tensor(dst[:, o:o + w], buf[:, pos:pos + w], T.gb[:, NC * i + o:NC * i + o + w], AluOpType.mult).then_inc(sem.mul, 1)
                    nm[0] += 1
                    pos += w

        v.wait_ge(sem.bc, 1)
        v.wait_ge(sem.pdo, 1)
        gate(T.po, oloc, me)
        for i, q in enumerate(P["rorder"][me]):
            v.wait_ge(sem["ra%d" % i], engines(unit[q], core, P["opos"][q, me][4]))
            gate(T.ret, P["rpos"][q, me], expert[q])
        v.wait_ge(sem.mul, nm[0])
        v.tensor_tensor(T.yb[:, :], T.yf[:, :], T.ys[:, :], AluOpType.add).then_inc(sem.add, 1)
        g.sync.wait_ge(sem.add, 1)
        g.sync.dma_start(T.y[:, :], T.yb[:, :]).then_inc(sem.yst, 16)
        g.sync.wait_ge(sem.yst, 16)
    g.wait_ge(sem.sent, sent[0])
